import numpy as np, ml_dtypes
CORES = [1,5,17,21,33,37,49,53]
N = 8
BF = ml_dtypes.bfloat16
def f(rng, *shape):
    return (rng.standard_normal(shape, dtype=np.float32) * np.exp2(rng.integers(-2, 3, shape[:-1] + (1,)))).astype(BF)
def wide(rng, *shape):
    v = f(rng, *shape).astype(np.float32); k = shape[:-2] + (1, shape[-1])
    return (v * np.exp2(rng.integers(-6, 7, k)) * (rng.random(k) > 0.0625)).astype(BF)
W, L, T, C, TH, SH = 4096, 192, 3, 5, 12, 12
def at(tab, a):
    return np.take_along_axis(tab, a.reshape(tab.shape[:-1] + (-1,)), -1).reshape(a.shape)
def tax(rng, key):
    term = np.argsort(key, axis=-1); gap = W - 1 - np.argsort(term, axis=-1)
    def up(lo, hi):
        v = np.where(rng.random((N, 8, W)) < 0.75, rng.random((1, 8, W)), rng.random((N, 8, W)))
        return np.take_along_axis(np.broadcast_to(term, (N, 8, W)), W - 1 - (gap * (lo + (hi - lo) * v)).astype(np.int64), 2)
    return term, gap, up(0.3, 0.7), up(0.05, 0.4)
def heights(rng, gap):
    h = (1.5 * (SH - np.log2(gap + 1.0))).astype(np.float32)[None, :, None, :]
    e = (h + rng.standard_normal((N, 8, 16, W), dtype=np.float32)) * np.exp2(rng.integers(-2, 3, (N, 8, 16, 1))).astype(np.float32)
    return e.reshape(N, 128, W).astype(BF)
def low(rng, term, n, top):
    return np.take_along_axis(np.broadcast_to(term, (N, 8, W)), rng.integers(0, top, (N, 8, n)), 2)
def lanes(rng, term, p0, p1):
    s = low(rng, term, 16 * L, W // 2).reshape(N, 8, 16, L)
    z = np.where(rng.random((N, 8, 16 * T * L)) < 0.1, low(rng, term, 16 * T * L, W), low(rng, term, 16 * T * L, W // 2)).reshape(N, 8, 16, T, L)
    kind = rng.integers(0, 8, (N, 8, 1, L))
    d = np.where(kind < 4, rng.integers(2, C + 1, s.shape), rng.integers(1, C + 1, s.shape)); d = np.where((kind < 3) & (rng.random(s.shape) < 0.1), 1, d)
    a = s
    for i in range(C):
        nx = at(p0, a)
        if i == 0: nx = np.where(rng.random(s.shape) < 0.4, at(p1, a), nx)
        a = np.where(d > i, nx, a)
    g = np.where(kind == 7, low(rng, term, 16 * L, W).reshape(s.shape), a)
    return s, g, z, (rng.random((N, 8, T, L)) < 0.4).astype(np.int64)
def pack(e, pa, s, g, z, sg):
    i4 = lambda v, *sh: np.ascontiguousarray(np.reshape(v, (N,) + sh)).astype(np.int32)
    return {"ev": np.reshape(e, (N, 128, W)).astype(BF), "par": i4(pa, 8, W), "s0": i4(s, 128, L), "g0": i4(g, 128, L), "z": i4(z, 128, T * L), "sg": i4(sg, 8, T * L)}
def setup_inputs(rng):
    term, gap, p0, p1 = tax(rng, rng.random((8, W)))
    return pack(heights(rng, gap), p0 + W * p1, *lanes(rng, term, p0, p1))
def setup_inputs_corners(rng):
    term, gap, p0, p1 = tax(rng, rng.random((8, W))); own = np.arange(W); c = rng.integers(0, 7, (1, 8, W))
    p0 = np.where(c == 0, own, np.where((c == 1) | (c == 4), W - 1, np.where((c == 2) | (c == 3), 0, p0)))
    p1 = np.where((c == 0) | (c == 3), own, np.where(c == 1, W - 1, np.where((c == 2) | (c == 4), 0, p1)))
    b = np.where(np.arange(N)[:, None, None] == 0, own, W - 1); p0 = np.where(c == 6, b, p0); p1 = np.where(c == 6, b, p1)
    for p in (p0, p1): p[:, ::2, W - 1] = W - 1; p[:, 1::2, W - 1] = 0
    e = heights(rng, gap).astype(np.float32); e[:, :, 0] = -256.0; e[:, :, W - 1] = 256.0
    s, g, z, sg = lanes(rng, term, p0, p1); one = (N, 8, 1, L)
    n = rng.choice(np.array([0, 0, 1, 4, 5, 16]), one); k = np.argsort(rng.random(s.shape), axis=2)
    g = np.where(rng.random(one) < 0.8, np.where(k < n, 0, W - 1), g)
    same = rng.random(one) < 0.2; s = np.where(same, s[:, :, :1], s); z = np.where(same[:, :, :, None], z[:, :, :1], z)
    g = np.where(rng.random(one) < 0.08, s, g); m = rng.integers(0, 8, (N, 8, 1, T, L))
    z = np.where(m == 0, s[:, :, :, None], np.where((m == 1) & (rng.random(z.shape) < 0.5), W - 1, np.where((m == 2) & (rng.random(z.shape) < 0.3), 0, z)))
    sg[0, :, 0] = 0; sg[1, :, 0] = 1; sg[2, :, 0] = 1; g[0] = W - 1
    for h in range(8):
        o = np.nonzero(c[0, h, 1:W - 1] == 0)[0] + 1; v = np.nonzero(c[0, h, 1:W - 1] == 6)[0] + 1
        s[0, h] = np.where(rng.random((1, L)) < 0.4, rng.choice(o, (16, L)), rng.choice(v, (16, L)))
        a, u = rng.permutation(v)[:2]; w = e[:, 16 * h:16 * h + 16]
        w[1:, :, a] = w[1:, :, u]; w[1, rng.permutation(16)[TH:], a] = -256.0
        j = np.append(rng.permutation(L - 1)[:L // 8], L - 1); i = rng.integers(0, 16, j.size)
        s[0, h, :, j] = rng.choice(o, (j.size, 16)); s[0, h, i, j] = a; z[0, h, i, 0, j] = u
    s[2, 7, :, L - 1] = rng.choice(o, 16); g[2, 7, :, L - 1] = W - 1; sg[2, 7, 0, L - 1] = 0
    for h in range(8):
        o = np.nonzero(c[0, h, 1:W - 1] == 0)[0] + 1; j = L if h < 7 else 1
        s[N - 1, h, :, :j] = rng.choice(o, (16, j)); g[N - 1, h, :, :j] = W - 1; sg[N - 1, h, 0] = 1; sg[N - 1, h, 0, :j] = 0
    return pack(e, p0 + W * p1, s, g, z, sg)
def setup_inputs_ends(rng):
    term, gap, p0, p1 = tax(rng, rng.random((8, W))); e = heights(rng, gap).astype(np.float32).reshape(N, 8, 16, W)
    cnt = rng.choice(np.array([0, 16, 8, 7, TH, TH - 1]), (N, 8, 1)); cnt[:, 0] = 16; cnt[:, 7] = 0
    v = np.where(np.argsort(rng.random((N, 8, 16)), axis=2) < cnt, 32.0, -32.0); v[:, 3] = 0.0
    e[..., 0] = v; e[..., W - 1] = -v
    pa = np.where(rng.random((N, 8, W)) < 0.85, (W * W - 1) * rng.integers(0, 2, (N, 8, W)), p0 + W * p1)
    kind = rng.integers(0, 5, (N, 8)); kind[:, 0] = 0; kind[:, 7] = 0; kind[N - 1] = 2
    pa[:, :, 0] = np.array([W * W - 1, 0, W * W - 1, 0, W - 1])[kind]; pa[:, :, W - 1] = np.array([0, W * W - 1, W * W - 1, 0, W * (W - 1)])[kind]
    def ends(*t):
        sh = (N, 8, 16) + t + (L,); one = (N, 8, 1) + t + (L,)
        x = np.where(rng.random(one) < 0.5, (W - 1) * rng.integers(0, 2, one), (W - 1) * rng.integers(0, 2, sh))
        return np.where((rng.random(one) < 0.25) & (rng.random(sh) < 0.5), rng.integers(0, W, sh), x)
    s = ends(); g = ends(); z = ends(T); sg = rng.integers(0, 2, (N, 8, T, L))
    x = (W - 1) * rng.integers(0, 2, (8, 16, L)); s[N - 1] = x; g[N - 1] = x; z[N - 1, :, :, 0] = x; sg[N - 1, :, 0] = 0; sg[1, :, 0] = 1
    s[:N - 1, 7, :, L - 3:] = 0; g[:N - 1, 7, :, L - 2:] = W - 1; g[:N - 1, 7, :, L - 3] = 0
    z[:N - 1, 7, :, 0, L - 3:] = W - 1; z[:N - 1, 7, :15, 0, L - 1] = 0; sg[:N - 1, 7, 0, L - 3:] = np.array([1, 0, 0])
    return pack(e, pa, s, g, z, sg)
def setup_inputs_spread(rng):
    c = rng.integers(-6, 7, (8, W)); term, gap, p0, p1 = tax(rng, c + rng.random((8, W)))
    w = np.abs(wide(rng, N, 128, W).astype(np.float32)).reshape(N, 8, 16, W) * np.exp2(2.0 * c).astype(np.float32)[None, :, None, :]
    w = np.where(rng.random((N, 8, 16, 1)) < 0.06, -w, w)
    return pack(w, p0 + W * p1, *lanes(rng, term, p0, p1))
def setup_inputs_ties(rng):
    term, gap, p0, p1 = tax(rng, rng.random((8, W))); q = W // 8; top = gap < q
    x = rng.integers(0, 4, (N, 8, 16, W)); x = np.where(top[None, :, None, :] & (rng.random(x.shape) < 0.75), 3, x)
    x[:, 5] = x[:, 5] // 2; x[:, 2] = 1
    u = np.take_along_axis(term[:, W - q:], rng.integers(0, q, (8, W)), 1)[None]
    p0 = np.where(rng.random((N, 8, W)) < 0.9, u, p0); p1 = np.where(rng.random((1, 8, W)) < 0.6, p0, p1)
    s, g, z, sg = lanes(rng, term, p0, p1); g = np.where(rng.random((N, 8, 1, L)) < 0.7, at(p0, s), g)
    return pack(x.astype(np.float32), p0 + W * p1, s, g, z, sg)
def check_inputs(d):
    bad = []
    for k, hi in (("par", W * W - 1), ("s0", W - 1), ("g0", W - 1), ("z", W - 1), ("sg", 1)):
        if np.min(d[k]) < 0 or np.max(d[k]) > hi: bad.append("range of " + k)
    e = d["ev"].astype(np.float32)
    if not np.all(np.isfinite(e)): bad.append("ev is not finite")
    if np.any((e != 0) & (np.abs(e) < np.float32(2.0 ** -126))): bad.append("ev holds subnormal numbers")
    return bad
def wits(tab, a):
    return np.take_along_axis(tab, a.reshape(8, 1, -1), 2).reshape(8, 16, 16, L)
def reference(ev, par, s0, g0, z, sg):
    e = ev.astype(np.float32).reshape(N, 8, 16, W); pa = par.astype(np.int64); p0 = pa & (W - 1); p1 = pa >> SH
    zs = z.astype(np.int64).reshape(N, 8, 16, T, L); plus = sg.reshape(N, 8, T, L) == 1
    S = s0.astype(np.int64).reshape(N, 8, 16, L); G = g0.astype(np.int64).reshape(N, 8, 16, L)
    ride = np.zeros((N, 8, L), bool); rz = np.zeros((N, 8, 16, L), np.int64)
    for t in range(T):
        for r in range(N):
            q = (r + t) % N; th = TH + (int(np.sum(ride[r])) & 1)
            x = np.where(ride[r][:, None], rz[r], zs[q, :, :, t]); pos = (plus[q, :, t] & ~ride[r])[:, None]
            ex = wits(e[q], x); g = G[r]; a = S[r]
            miss = np.sum(np.sum(wits(e[q], g) >= ex, axis=1) < th, axis=1)[:, None]
            for i in range(C):
                cov = np.sum(wits(e[q], a) >= ex, axis=1)
                nx = np.where(cov >= 8, at(p0[q], a), at(p1[q], a))
                stop = np.where(pos, cov >= th, nx == g)
                a = np.where(stop, a, nx)
            full = ~pos & (miss == 0); can = full & stop & (cov < th)
            win = np.argmin(np.where(can, cov, 99), axis=1)
            hit = can & (np.arange(16)[None, :, None] == win[:, None])
            S[r] = np.where(pos, a, S[r]); G[r] = np.where((pos & (miss > 4)) | hit, a, g)
            ride[r] = full[:, 0] & ~np.any(can, axis=1); rz[r] = x
    return {"ys": S.reshape(N, 128, L).astype(np.float32), "yg": G.reshape(N, 128, L).astype(np.float32)}

@@ -1,0 +1,517 @@
+import math
+from concourse.mybir import AluOpType, AxisListType, ActivationFunctionType
+
+A = AluOpType
+F = ActivationFunctionType
+NR, W, L, VIS, CL = 8, 4096, 192, 3, 5
+NCH = 3
+NL = L // NCH
+J = 16 * NL
+BIG = float(2 ** 22)
+LN2 = math.log(2.0)
+MIX = {"skew": 1.0, "slack": 0.12, "g": 1.5, "pe": 0.42, "hop": 0.08, "ecv": 1, "remote": 3.0, "th": 40.0, "track": 0.0, "gcov": 0.0}
+
+ZM = ["PO", "TT", "MS", "G1", "G2", "CF", "NC", "W2", "UU", "CGV"] + ["E%d" % i for i in range(CL)] + ["F%d" % i for i in range(CL)]
+ZI_ = ["MI", "XI", "CI"]
+SCALED = {"IB": 1.0, "NIB": -1.0, "I2K": 2048.0, "N2K": -2048.0, "I8K": 8192.0, "NHB": -BIG / 2, "NB": -BIG, "I16K": 16384.0, "I32B": 32.0}
+SEL = ["BOA", "BOF", "E8A", "E8F"]
+
+SCRATCH = {
+    "EVB": ("sbuf", [128, W], "bfloat16"), "EC": ("sbuf", [128, 2 * W], "bfloat16"), "DT": ("sbuf", [128, 2 * W], "bfloat16"),
+    "PN": ("sbuf", [128, 256], "int32"), "PT": ("sbuf", [128, 16, 16], "int32"), "PF": ("sbuf", [128, 256], "float32"),
+    "TR": ("sbuf", [128, 256], "float32"), "TI": ("sbuf", [128, 256], "int32"), "TA": ("sbuf", [128, 512], "int32"),
+    "PL": ("sbuf", [128, 512], "uint16"),
+    "DGI": ("sbuf", [128, 1024], "int32"), "DGB": ("sbuf", [128, 1024], "bfloat16"),
+    "S0I": ("sbuf", [128, L], "int32"), "G0I": ("sbuf", [128, L], "int32"), "ZI": ("sbuf", [128, VIS * L], "int32"),
+    "SG8": ("sbuf", [128, VIS * L], "int32"), "SG8B": ("sbuf", [128, VIS * L], "bfloat16"), "SGB": ("sbuf", [128, VIS * L], "bfloat16"),
+    "ONE": ("sbuf", [128, 128], "float32"), "I32": ("sbuf", [128, 128], "float32"),
+    "ON16": ("sbuf", [128, 128], "float32"), "SEL": ("sbuf", [128, 128 * len(SEL)], "float32"), "SCN": ("sbuf", [128, 128 * len(SCALED)], "bfloat16"),
+    "BO": ("sbuf", [128, 128], "bfloat16"), "BOH": ("sbuf", [128, 128], "bfloat16"), "E8": ("sbuf", [128, 128], "bfloat16"),
+    "WK": ("sbuf", [128, 2048], "bfloat16"),
+    "KI": ("sbuf", [128, 2], "int32"), "KB": ("sbuf", [128, 2], "float32"), "RS": ("sbuf", [128, 2], "float32"), "THI": ("sbuf", [128, 4], "int32"),
+    "VB": ("psum", [128, 512], "float32"), "PB": ("psum", [128, 512], "float32"),
+}
+for _t in range(VIS):
+    SCRATCH["ZU%d" % _t] = ("sbuf", [128, L], "uint16")
+    SCRATCH["TH%d" % _t] = ("sbuf", [128, 2], "float32")
+    if _t:
+        for _n, _d in (("ZR", "uint16"), ("ZF", "float32"), ("DZ", "float32"), ("NRL", "bfloat16"), ("NRS", "bfloat16")):
+            SCRATCH["%s%d" % (_n, _t)] = ("sbuf", [128, L], _d)
+SEMAPHORES = ["qV", "qS", "qT", "qG", "lsend", "zr1", "zr2"]
+for _c in range(NCH):
+    for _n, _k, _d in (("US", 2 * NL, "uint16"), ("IDX", NL, "uint16"), ("EX", J, "bfloat16"), ("CG", J, "bfloat16"), ("CM", J, "bfloat16"), ("DG", J, "bfloat16"),
+                       ("IH", 6 * NL, "float32"), ("SH", 6 * NL, "bfloat16"), ("CH", 6 * NL, "bfloat16"), ("MM", NL, "float32"),
+                       ("SM", NL * len(ZM), "bfloat16"), ("SI", NL * len(ZI_), "int32")):
+        SCRATCH["%s%d" % (_n, _c)] = ("sbuf", [128, _k], _d)
+    for _n in ("BC", "BM"):
+        SCRATCH["%s%d" % (_n, _c)] = ("psum", [128, 512], "float32")
+    for _t in range(VIS + 1):
+        SCRATCH["L%d_%d" % (_t, _c)] = ("sbuf", [128, 2 * NL], "float32")
+        if _t:
+            SCRATCH["X%d_%d" % (_t, _c)] = ("sbuf", [128, 2 * NL], "float32")
+            SEMAPHORES.append("aL%d_%d" % (_t, _c))
+            if _t < VIS:
+                SEMAPHORES.append("aN%d_%d" % (_t, _c))
+DMAS = ["PTa", "PTb", "PN", "EV", "Z0", "Z1", "S0", "G0", "SG", "D0", "D1", "D2", "D3"] + ["o%s%d" % (x, c) for x in "sg" for c in range(NCH)]
+SEMAPHORES += ["d_" + n for n in DMAS]
+PSUM = {n for n in SCRATCH if SCRATCH[n][0] == "psum" and n != "VB"}
+ACOL = 256
+CY = 0.00083
+
+
+def vc(n):
+    return max(64, n) * CY + 0.02
+
+
+def sc(n):
+    return max(64, n) * CY + 0.04
+
+
+def ga(n):
+    return 0.055 + n * CY * MIX["g"]
+
+
+def pc(cycles):
+    return cycles * MIX["pe"] * 1e-3 + 0.03
+
+
+def al(n, lo=0, hi=None):
+    if n in SCALED:
+        i = list(SCALED).index(n)
+        return ("SCN", i * 128, i * 128 + 128)
+    if n in SEL:
+        i = SEL.index(n)
+        return ("SEL", i * 128, i * 128 + 128)
+    return (n, lo, SCRATCH[n][1][-1] if hi is None else hi)
+
+
+def cst(T, n):
+    b, lo, hi = al(n)
+    return T[b][:, lo:hi]
+
+
+def zr(n, c):
+    b, l = ("SM", ZM) if n in ZM else ("SI", ZI_)
+    i = l.index(n)
+    return ("%s%d" % (b, c), i * NL, i * NL + NL)
+
+
+def z(T, n, c):
+    b, lo, hi = zr(n, c)
+    return T[b][:, lo:hi]
+
+
+def build():
+    ops = []
+
+    def op(q, cost, R, Wr, f, key, done=None, frm=None, bonus=0.0):
+        ops.append({"q": q, "cost": cost, "R": R, "W": Wr, "f": f, "key": key, "done": done, "frm": frm, "bonus": bonus})
+
+    def V(n, R, Wr, f, key, bonus=0.0):
+        op("V", vc(n), R, Wr, f, key, bonus=bonus)
+
+    def S(n, R, Wr, f, key, bonus=0.0):
+        op("S", sc(n), R, Wr, f, key, bonus=bonus)
+
+    def load(q, sem, R, Wr, f, cost, key=(-1, 0)):
+        op(q, cost, R, Wr, f, key, done="d_" + sem)
+
+    K0 = (-1, 0)
+    for y in range(2):
+        load("Y", "PT" + "ab"[y], [], [("PT", y, y + 1)], lambda g, T, x, y=y: g.sync.dma_start(T.PT[:, y:16:2, :], T.par[y:8:2, :]), 3.0)
+    load("S", "S0", [], [al("S0I")], lambda g, T, x: g.scalar.dma_start(T.S0I[:], T.s0[:]), 2.4)
+    load("S", "Z0", [], [al("ZI", 0, L)], lambda g, T, x: g.scalar.dma_start(T.ZI[:, 0:L], T.z[:, 0:L]), 2.4)
+    load("S", "G0", [], [al("G0I")], lambda g, T, x: g.scalar.dma_start(T.G0I[:], T.g0[:]), 2.6)
+    load("Y", "PN", [], [al("PN")], lambda g, T, x: g.sync.dma_start(T.PN[:], T.par[:]), 3.2)
+    load("Y", "EV", [], [al("EVB")], lambda g, T, x: g.sync.dma_start(T.EVB[:], T.ev[:]), 8.0)
+    load("S", "SG", [], [al("SG8")], lambda g, T, x: g.scalar.dma_start(T.SG8[0:8, :], T.sg[:]), 3.0)
+    load("Y", "Z1", [], [al("ZI", L, VIS * L)], lambda g, T, x: g.sync.dma_start(T.ZI[:, L:VIS * L], T.z[:, L:VIS * L]), 10.0, (0, 9))
+
+    V(128, [], [al("ONE")], lambda g, T, x: g.vector.memset(T.ONE[:], 1.0), K0, bonus=50.0)
+
+    def asel(o, i, pat, cmp, base, ch):
+        oa = lambda T: T.I32[:] if o == "I32" else cst(T, o)
+        ia = lambda T: T.ONE[:] if i == "ONE" else cst(T, i)
+        op("G", 0.4, [al(i)], [al(o)], lambda g, T, x: g.affine_select(oa(T), ia(T), pat, cmp, 0.0, base, ch), K0, bonus=40.0)
+    asel("I32", "ONE", [[-1, 128]], A.is_equal, 0, 1)
+    asel("BOA", "ONE", [[-16, 8], [0, 16]], A.is_ge, 0, 1)
+    asel("BOF", "BOA", [[16, 8], [0, 16]], A.is_ge, 15, -1)
+    asel("E8A", "ONE", [[1, 128]], A.is_ge, 0, -16)
+    asel("E8F", "E8A", [[-1, 128]], A.is_ge, 15, 16)
+    op("G", 7.0, [], [al("DT", 0, W)], lambda g, T, x: g.iota(T.DT[:, 0:W], [[0, W]], 0, 0, allow_small_or_imprecise_dtypes=True), K0, bonus=30.0)
+    op("G", 0.15, [], [al("KI", 0, 1)], lambda g, T, x: g.iota(T.KI[:, 0:1], [[0, 1]], 0, 1), K0)
+    V(1, [al("KI", 0, 1)], [al("KI", 1, 2)], lambda g, T, x: g.vector.tensor_scalar(T.KI[:, 1:2], T.KI[:, 0:1], 15, None, A.bitwise_and), (0, 8))
+    V(1, [al("KI", 1, 2)], [al("KB", 0, 1)], lambda g, T, x: g.vector.tensor_scalar(T.KB[:, 0:1], T.KI[:, 1:2], -LN2, 94.0 * LN2, A.mult, A.add), (0, 8))
+    V(2048, [], [al("DT", W, 2 * W)], lambda g, T, x: g.vector.memset(T.DT[:, W:2 * W], 0.0), K0)
+    for k in range(16):
+        S(128, [al("I32")], [al("WK", k * 128, k * 128 + 128)], lambda g, T, x, k=k: g.scalar.activation(T.WK[:, k * 128:k * 128 + 128], T.I32[:], F.Copy, scale=0.0), K0)
+    for k in range(16):
+        S(8, [al("BOF")], [al("WK", k * 128, k * 128 + 128)], lambda g, T, x, k=k: g.scalar.activation(
+            T.WK[:, k * 128 + k:k * 128 + 128:16], T.SEL[:, 128 + k:256:16], F.Copy), K0)
+    for n in SCALED:
+        S(128, [al("I32")], [al(n)], lambda g, T, x, n=n: g.scalar.activation(cst(T, n), T.I32[:], F.Copy, scale=SCALED[n]), K0)
+    S(128, [al("E8F")], [al("E8")], lambda g, T, x: g.scalar.activation(T.E8[:], cst(T, "E8F"), F.Copy), K0)
+    S(128, [al("BOF")], [al("BO")], lambda g, T, x: g.scalar.activation(T.BO[:], cst(T, "BOF"), F.Copy), K0)
+    S(128, [al("BOF")], [al("BOH")], lambda g, T, x: g.scalar.activation(T.BOH[:], cst(T, "BOF"), F.Copy, scale=0.5), K0)
+    V(128, [], [al("ON16")], lambda g, T, x: g.vector.memset(T.ON16[:], 0.0625), (0, 8))
+    V(1, [], [al("TH0", 0, 1)], lambda g, T, x: g.vector.memset(T.TH0[:, 0:1], 12.0), (0, 8))
+    V(1, [], [al("TH0", 1, 2)], lambda g, T, x: g.vector.memset(T.TH0[:, 1:2], -87.0), (0, 8))
+    for c in range(NCH):
+        V(NL, [], [al("SH%d" % c, 5 * NL)], lambda g, T, x, c=c: g.vector.memset(T["SH%d" % c][:, 5 * NL:6 * NL], -1.0), (0, 8))
+        V(NL, [], [al("CH%d" % c, 5 * NL)], lambda g, T, x, c=c: g.vector.memset(T["CH%d" % c][:, 5 * NL:6 * NL], 191.0), (0, 8))
+
+    V(L, [al("ZI", 0, L)], [al("ZU0")], lambda g, T, x: g.vector.tensor_copy(T.ZU0[:], T.ZI[:, 0:L]), K0)
+    V(256, [("PT", 0, 16)], [al("PF")], lambda g, T, x: g.vector.tensor_copy(T.PF[:], T.PT[:]), K0)
+    V(256, [al("PF")], [al("TR")], lambda g, T, x: g.vector.transpose(T.TR[:], T.PF[:]), K0)
+    for q3 in range(8):
+        V(32, [al("TR")], [("TI", q3, q3 + 1)], lambda g, T, x, q3=q3: g.vector.tensor_copy(T.TI[:, q3:256:8], T.TR[:, q3 * 32:q3 * 32 + 32]), K0)
+    V(256, [al("TI")], [al("TA", 0, 256)], lambda g, T, x: g.vector.tensor_scalar(T.TA[:, 0:256], T.TI[:], 4095, None, A.bitwise_and), K0)
+    V(256, [al("TI")], [al("TA", 256, 512)], lambda g, T, x: g.vector.tensor_scalar(T.TA[:, 256:512], T.TI[:], 12, None, A.logical_shift_right), K0)
+    for h in range(2):
+        V(256, [al("TA", h * 256, h * 256 + 256)], [al("PL", h * 256, h * 256 + 256)], lambda g, T, x, h=h: g.vector.tensor_copy(
+            T.PL[:, h * 256:h * 256 + 256], T.TA[:, h * 256:h * 256 + 256]), K0)
+    for b, (sh, m) in enumerate(((0, 4032), (0, 63), (12, 4032), (12, 63))):
+        lo, hi = b * 256, b * 256 + 256
+        if sh:
+            V(256, [al("PN")], [al("DGI", lo, hi)], lambda g, T, x, lo=lo, hi=hi, sh=sh, m=m: g.vector.tensor_scalar(
+                T.DGI[:, lo:hi], T.PN[:], sh, m, A.logical_shift_right, A.bitwise_and), (0, 5))
+        else:
+            V(256, [al("PN")], [al("DGI", lo, hi)], lambda g, T, x, lo=lo, hi=hi, m=m: g.vector.tensor_scalar(
+                T.DGI[:, lo:hi], T.PN[:], m, None, A.bitwise_and), (0, 5))
+    V(1024, [al("DGI")], [al("DGB")], lambda g, T, x: g.vector.tensor_copy(T.DGB[:], T.DGI[:]), (0, 5))
+    for b in range(4):
+        load("Y", "D%d" % b, [al("DGB", b * 256, b * 256 + 256)], [("DT", (b // 2) * W, (b // 2) * W + W)], lambda g, T, x, b=b: g.sync.dma_start(
+            T.DT[b % 2:128:16, (b // 2) * W:(b // 2) * W + W], T.DGB[:, b * 256:b * 256 + 256]), 2.5, (0, 5))
+    V(576, [al("SG8")], [al("SG8B")], lambda g, T, x: g.vector.tensor_copy(T.SG8B[0:8, :], T.SG8[0:8, :]), (0, 6))
+    for t in range(VIS):
+        op("T", 0.1, [al("E8"), al("SG8B")], [al("PB", 0, L)], lambda g, T, x, t=t: g.tensor.matmul(T.PB[:, 0:L], T.E8[0:8, :], T.SG8B[0:8, t * L:t * L + L], True, True), (t, 6))
+        S(L, [al("PB", 0, L)], [al("SGB", t * L, t * L + L)], lambda g, T, x, t=t: g.scalar.activation(T.SGB[:, t * L:t * L + L], T.PB[:, 0:L], F.Copy), (t, 6))
+    for b in range(4):
+        R = [al("EVB"), al("PL", b * 128, b * 128 + 128)]
+        Wr = [al("EC", b * 2048, b * 2048 + 2048)]
+        if b < MIX["ecv"]:
+            op("V", ga(2048), R, Wr, lambda g, T, x, b=b: g.vector.tensor_copy(
+                T.EC[:, b * 2048:b * 2048 + 2048], T.EVB[:, 0:W].indirect(T.PL[:, b * 128:b * 128 + 128])), (0, 4))
+        else:
+            op("S", ga(2048), R, Wr, lambda g, T, x, b=b: g.scalar.activation(
+                T.EC[:, b * 2048:b * 2048 + 2048], T.EVB[:, 0:W].indirect(T.PL[:, b * 128:b * 128 + 128]), F.Copy), (0, 4))
+
+    def fold16(bank, col, src, stop=True):
+        def f(g, T, x):
+            for r in range(16):
+                y = g.tensor.matmul(T[bank][:, col:col + NL], T.WK[:, r * 128:r * 128 + 128], T[src][:, r:J:16], r == 0, r == 15 and stop)
+            return y
+        return f
+
+    def walk(t, c):
+        k = (t, c)
+        o, e = c * NL, "%d" % c
+        Ln, Un, ex, cm, cg, bank, dg, ix, zu = "L%d_%d" % (t, c), "US" + e, "EX" + e, "CM" + e, "CG" + e, "BC" + e, "DG" + e, "IDX" + e, "ZU%d" % t
+        vb = c * 2 * NL
+        if t == 0:
+            for h, n in enumerate(("S0I", "G0I")):
+                V(NL, [al(n, o, o + NL)], [al(Ln, h * NL, h * NL + NL)], lambda g, T, x, h=h, n=n: g.vector.tensor_copy(T[Ln][:, h * NL:h * NL + NL], T[n][:, o:o + NL]), k)
+            V(NL, [al("SGB", o, o + NL)], [zr("PO", c)], lambda g, T, x: g.vector.tensor_copy(z(T, "PO", c), T.SGB[:, o:o + NL]), k)
+        else:
+            nr, zf, dz = "NRL%d" % t, "ZF%d" % t, "DZ%d" % t
+            V(2 * NL, [al(nr, o, o + NL), al(dz, o, o + NL)], [al("VB", vb, vb + NL)], lambda g, T, x: g.vector.tensor_tensor(
+                T.VB[:, vb:vb + NL], T[dz][:, o:o + NL], T[nr][:, o:o + NL], A.mult), k)
+            V(NL, [al("VB", vb, vb + NL), al(zf, o, o + NL)], [al("VB", vb + NL, vb + 2 * NL)], lambda g, T, x: g.vector.tensor_tensor(
+                T.VB[:, vb + NL:vb + 2 * NL], T.VB[:, vb:vb + NL], T[zf][:, o:o + NL], A.add), k)
+            V(NL, [al("VB", vb + NL, vb + 2 * NL)], [al(zu, o, o + NL)], lambda g, T, x: g.vector.tensor_copy(T[zu][:, o:o + NL], T.VB[:, vb + NL:vb + 2 * NL]), k)
+            op("R", MIX["remote"], [al("X%d_%d" % (t, c))], [al(Ln)], None, k, done="aL%d_%d" % (t, c), frm=-1)
+            V(2 * NL, [al("SGB", t * L + o, t * L + o + NL), al(nr, o, o + NL)], [zr("PO", c)], lambda g, T, x: g.vector.tensor_tensor(
+                z(T, "PO", c), T.SGB[:, t * L + o:t * L + o + NL], T[nr][:, o:o + NL], A.mult), k)
+        V(2 * NL, [al(Ln)], [al(Un)], lambda g, T, x: g.vector.tensor_copy(T[Un][:], T[Ln][:]), k)
+        op("S", ga(J), [al("EVB"), al(zu, o, o + NL)], [al(ex)], lambda g, T, x: g.scalar.activation(T[ex][:], T.EVB[:, 0:W].indirect(T[zu][:, o:o + NL]), F.Copy), k)
+        op("V", ga(J), [al("EVB"), al(Un), al(ex)], [al(cm)], lambda g, T, x: g.vector.tensor_tensor(
+            T[cm][:], T.EVB[:, 0:W].indirect(T[Un][:, 0:NL]), T[ex][:], A.is_ge), k)
+        ih, ch, sh = "IH" + e, "CH" + e, "SH" + e
+        aw = (bank, ACOL, ACOL + NL)
+        for i in range(CL + 1):
+            lo, hi = i * NL, i * NL + NL
+            if i:
+                if i < CL:
+                    op("V", ga(J), [al("EC"), al(ix), al(ex)], [al(cm)], lambda g, T, x: g.vector.tensor_tensor(
+                        T[cm][:], T.EC[:, 0:2 * W].indirect(T[ix][:]), T[ex][:], A.is_ge), k)
+                op("S", ga(J), [al("DT"), al(ix)], [al(dg)], lambda g, T, x: g.scalar.activation(T[dg][:], T.DT[:, 0:2 * W].indirect(T[ix][:]), F.Copy), k)
+            if i < CL:
+                op("T", pc(J), [al("WK"), al(cm)], [al(bank, 0, NL)], fold16(bank, 0, cm), k)
+            if i:
+                op("T", pc(J), [al("WK"), al(dg)], [aw], fold16(bank, ACOL, dg, i == CL), k)
+            else:
+                op("T", pc(4 * NL), [al("I32"), al(Ln, 0, NL)], [aw], lambda g, T, x: g.tensor.matmul(T[bank][:, ACOL:ACOL + NL], T.I32[:], T[Ln][:, 0:NL], True, False), k)
+            if i == CL:
+                S(NL, [aw], [al(ih, lo, hi)], lambda g, T, x, lo=lo, hi=hi: g.scalar.activation(T[ih][:, lo:hi], T[bank][:, ACOL:ACOL + NL], F.Identity, bias=-2048.0), k)
+                break
+            S(NL, [al(bank, 0, NL)], [al(sh, lo, hi)], lambda g, T, x, lo=lo, hi=hi: g.scalar.activation(T[sh][:, lo:hi], T[bank][:, 0:NL], F.Sign, bias=7.5, scale=-1.0), k)
+            S(NL, [al(bank, 0, NL)], [al(ch, lo, hi)], lambda g, T, x, lo=lo, hi=hi, i=i: g.scalar.activation(
+                T[ch][:, lo:hi], T[bank][:, 0:NL], F.Identity, bias=32.0 * i), k)
+            op("T", pc(NL), [al("I2K"), al(sh, lo, hi)], [aw], lambda g, T, x, lo=lo, hi=hi: g.tensor.matmul(
+                T[bank][:, ACOL:ACOL + NL], cst(T, "I2K"), T[sh][:, lo:hi], False, True), k)
+            V(NL, [aw], [al(ix)], lambda g, T, x: g.vector.tensor_scalar(T[ix][:], T[bank][:, ACOL:ACOL + NL], 2048.0, None, A.add), k)
+            S(NL, [aw], [al(ih, lo, hi)], lambda g, T, x, lo=lo, hi=hi: g.scalar.activation(T[ih][:, lo:hi], T[bank][:, ACOL:ACOL + NL], F.Copy), k)
+            if i == 0:
+                op("V", ga(J), [al("EVB"), al(Un), al(ex)], [al(cg)], lambda g, T, x: g.vector.tensor_tensor(
+                    T[cg][:], T.EVB[:, 0:W].indirect(T[Un][:, NL:2 * NL]), T[ex][:], A.is_ge), k, bonus=MIX["gcov"])
+                op("T", pc(J), [al("WK"), al(cg)], [al("BM" + e, 0, NL)], fold16("BM" + e, 0, cg), k)
+                S(NL, [al("BM" + e, 0, NL)], [zr("CGV", c)], lambda g, T, x: g.scalar.activation(z(T, "CGV", c), T["BM" + e][:, 0:NL], F.Copy), k)
+
+    def epilogue(t, c):
+        k = (t, c)
+        e = "%d" % c
+        bm, th, Ln, ih, ch, mmn, sh = "BM" + e, "TH%d" % t, "L%d_%d" % (t, c), "IH" + e, "CH" + e, "MM" + e, "SH" + e
+        tb = MIX["track"]
+
+        def Z(n):
+            return zr(n, c)
+        bk = al(bm, 0, NL)
+        V(NL, [Z("PO"), al(th)], [Z("TT")], lambda g, T, x: g.vector.tensor_scalar(z(T, "TT", c), z(T, "PO", c), T[th][:, 1:2], 99.0, A.mult, A.add), k)
+        V(NL, [Z("CGV"), al(th)], [Z("MS")], lambda g, T, x: g.vector.tensor_scalar(z(T, "MS", c), z(T, "CGV", c), T[th][:, 0:1], None, A.is_lt), k)
+
+        def fr(g, T, x):
+            g.tensor.matmul(T[bm][:, 0:NL], T.BO[:], z(T, "MS", c), True, False)
+            return g.tensor.matmul(T[bm][:, 0:NL], cst(T, "I32B"), z(T, "PO", c), False, True)
+        op("T", pc(2 * NL), [al("BO"), al("I32B"), Z("MS"), Z("PO")], [bk], fr, k)
+        V(NL, [bk], [Z("G1")], lambda g, T, x: g.vector.tensor_scalar(z(T, "G1", c), T[bm][:, 0:NL], 0.5, 2.0 ** 98, A.is_ge, A.mult), k)
+        V(NL, [bk], [Z("G2")], lambda g, T, x: g.vector.tensor_scalar(z(T, "G2", c), T[bm][:, 0:NL], 36.5, -(2.0 ** 99), A.is_ge, A.mult), k)
+        for i in range(CL):
+            s0, s1 = slice(i * NL, i * NL + NL), slice((i + 1) * NL, (i + 2) * NL)
+            En, Fn = "E%d" % i, "F%d" % i
+
+            def fy(g, T, x, s0=s0, s1=s1):
+                g.tensor.matmul(T[bm][:, NL:2 * NL], cst(T, "IB"), T[ch][:, s0], True, False)
+                g.tensor.matmul(T[bm][:, NL:2 * NL], cst(T, "NIB"), z(T, "TT", c), False, True)
+                g.tensor.matmul(T[bm][:, 0:NL], T.I32[:], T[ih][:, s1], True, False)
+                g.tensor.matmul(T[bm][:, 0:NL], cst(T, "N2K"), T[sh][:, s1], False, False)
+                return g.tensor.matmul(T[bm][:, 0:NL], cst(T, "I16K"), z(T, "PO", c), False, True)
+            op("T", pc(8 * NL), [al("I32"), al("I16K"), al("N2K"), al(sh, s1.start, s1.stop), al("IB"), al("NIB"), al(ih, s1.start, s1.stop), Z("PO"), al(ch, s0.start, s0.stop), Z("TT")], [al(bm, 0, 2 * NL)], fy, k, bonus=tb)
+            V(NL, [bk, al(Ln, NL, 2 * NL)], [Z(En)], lambda g, T, x, En=En: g.vector.tensor_tensor(z(T, En, c), T[bm][:, 0:NL], T[Ln][:, NL:2 * NL], A.is_equal), k, bonus=tb)
+            S(NL, [al(bm, NL, 2 * NL)], [Z(Fn)], lambda g, T, x, Fn=Fn, i=i: g.scalar.activation(z(T, Fn, c), T[bm][:, NL:2 * NL], F.Sign, bias=0.5 - 32.0 * i), k, bonus=tb)
+            last = i == CL - 1
+
+            def fw(g, T, x, s0=s0, s1=s1, En=En, Fn=Fn, last=last):
+                if last:
+                    g.tensor.matmul(T[bm][:, NL:2 * NL], T.I32[:], T[ih][:, s1], True, False)
+                    g.tensor.matmul(T[bm][:, NL:2 * NL], cst(T, "I8K"), T[ch][:, s1], False, True)
+                g.tensor.matmul(T[bm][:, 0:NL], T.I32[:], T[ih][:, s0], True, False)
+                g.tensor.matmul(T[bm][:, 0:NL], cst(T, "I8K"), T[ch][:, s0], False, False)
+                g.tensor.matmul(T[bm][:, 0:NL], cst(T, "NHB"), z(T, Fn, c), False, False)
+                return g.tensor.matmul(T[bm][:, 0:NL], cst(T, "NB"), z(T, En, c), False, True)
+            op("T", pc((12 if last else 7) * NL), [al("I32"), al("I8K"), al("NHB"), al("NB"), al(ih, s0.start, s1.stop), al(ch, s0.start, s1.stop if last else s0.stop), Z(En), Z(Fn)],
+               [al(bm, 0, 2 * NL)], fw, k, bonus=tb)
+            if i == 0:
+                V(NL, [bk], [al(mmn)], lambda g, T, x: g.vector.tensor_copy(T[mmn][:], T[bm][:, 0:NL]), k, bonus=tb)
+            else:
+                for j in range(2 if last else 1):
+                    V(NL, [al(bm, j * NL, j * NL + NL), al(mmn)], [al(mmn)], lambda g, T, x, j=j: g.vector.tensor_tensor(
+                        T[mmn][:], T[bm][:, j * NL:j * NL + NL], T[mmn][:], A.min), k, bonus=tb)
+        V(NL, [al(mmn)], [Z("MI")], lambda g, T, x: g.vector.tensor_scalar(z(T, "MI", c), T[mmn][:], 2048.0, None, A.add), k)
+        V(NL, [Z("MI")], [Z("CI")], lambda g, T, x: g.vector.tensor_scalar(z(T, "CI", c), z(T, "MI", c), 13, 31, A.arith_shift_right, A.bitwise_and), k)
+        V(NL, [Z("CI"), al(th)], [Z("NC")], lambda g, T, x: g.vector.tensor_scalar(z(T, "NC", c), z(T, "CI", c), T[th][:, 0:1], 64.0, A.is_ge, A.mult), k)
+        V(NL, [Z("CI")], [Z("CF")], lambda g, T, x: g.vector.tensor_copy(z(T, "CF", c), z(T, "CI", c)), k)
+        V(NL, [Z("MI")], [Z("XI")], lambda g, T, x: g.vector.tensor_scalar(z(T, "XI", c), z(T, "MI", c), 4095, None, A.bitwise_and), k)
+
+        def fc(g, T, x):
+            g.tensor.matmul(T[bm][:, 0:NL], cst(T, "IB"), z(T, "NC", c), True, False)
+            return g.tensor.matmul(T[bm][:, 0:NL], cst(T, "IB"), z(T, "CF", c), False, True)
+        op("T", pc(2 * NL), [al("IB"), Z("CF"), Z("NC")], [bk], fc, k)
+        S(NL, [bk, al("KB", 0, 1)], [Z("W2")], lambda g, T, x: g.scalar.activation(z(T, "W2", c), T[bm][:, 0:NL], F.Exp, bias=T.KB[:, 0:1], scale=-16.0 * LN2), k)
+
+        def fs(g, T, x):
+            g.tensor.matmul(T[bm][:, 0:NL], cst(T, "IB"), z(T, "G1", c), True, False)
+            g.tensor.matmul(T[bm][:, 0:NL], cst(T, "IB"), z(T, "G2", c), False, False)
+            return g.tensor.matmul(T[bm][:, 0:NL], T.BOH[:], z(T, "W2", c), False, True)
+        op("T", pc(3 * NL), [al("IB"), al("BOH"), Z("G1"), Z("G2"), Z("W2")], [bk], fs, k)
+        vb = c * 2 * NL
+        r0, r1 = (vb, vb + NL), (vb + NL, vb + 2 * NL)
+        Xn = "X%d_%d" % (t + 1, c)
+
+        def vt(in0, in1, out, alu, R, Wr):
+            V(NL, R, Wr, lambda g, T, x: g.vector.tensor_tensor(out(T), in0(T), in1(T), alu), k)
+
+        def vbs(r):
+            return lambda T: T.VB[:, r[0]:r[1]]
+        V(NL, [Z("XI")], [al("VB", *r0)], lambda g, T, x: g.vector.tensor_copy(T.VB[:, r0[0]:r0[1]], z(T, "XI", c)), k)
+        lS, lG = (lambda T: T[Ln][:, 0:NL]), (lambda T: T[Ln][:, NL:2 * NL])
+        vt(vbs(r0), lS, vbs(r1), A.subtract, [al("VB", *r0), al(Ln, 0, NL)], [al("VB", *r1)])
+        vt(vbs(r0), lG, vbs(r0), A.subtract, [al("VB", *r0), al(Ln, NL, 2 * NL)], [al("VB", *r0)])
+        vt(vbs(r1), lambda T: z(T, "PO", c), vbs(r1), A.mult, [al("VB", *r1), Z("PO")], [al("VB", *r1)])
+        vt(vbs(r1), lS, lambda T: T[Xn][:, 0:NL], A.add, [al("VB", *r1), al(Ln, 0, NL)], [al(Xn, 0, NL)])
+        o = c * NL
+        if t + 1 < VIS:
+            ns, nl = "NRS%d" % (t + 1), "NRL%d" % (t + 1)
+            V(NL, [bk], [al(ns, o, o + NL)], lambda g, T, x: g.vector.tensor_scalar(T[ns][:, o:o + NL], T[bm][:, 0:NL], 0.0, None, A.not_equal), k)
+            op("G", 0.1, [al(ns, o, o + NL)], [], lambda g, T, x: x["send"](T[nl][:, o:o + NL], T[ns][:, o:o + NL], "aN%d_%d" % (t + 1, c), "next"), k)
+            op("R", MIX["remote"], [al(ns, o, o + NL)], [al(nl, o, o + NL)], None, k, done="aN%d_%d" % (t + 1, c), frm=-1)
+        V(NL, [bk, Z("W2")], [Z("UU")], lambda g, T, x: g.vector.tensor_tensor(z(T, "UU", c), T[bm][:, 0:NL], z(T, "W2", c), A.is_lt), k)
+        vt(vbs(r0), lambda T: z(T, "UU", c), vbs(r0), A.mult, [al("VB", *r0), Z("UU")], [al("VB", *r0)])
+        vt(vbs(r0), lG, lambda T: T[Xn][:, NL:2 * NL], A.add, [al("VB", *r0), al(Ln, NL, 2 * NL)], [al(Xn, NL, 2 * NL)])
+        if t + 1 < VIS:
+            op("G", 0.1, [al(Xn)], [], lambda g, T, x: x["send"](T["L%d_%d" % (t + 1, c)][:], T[Xn][:], "aL%d_%d" % (t + 1, c), "next"), k)
+        else:
+            H = "L%d_%d" % (VIS, c)
+            op("G", 0.1, [al(Xn)], [], lambda g, T, x: x["send"](T[H][:], T[Xn][:], "aL%d_%d" % (VIS, c), "home"), k)
+            op("R", MIX["remote"], [al(Xn)], [al(H)], None, k, done="aL%d_%d" % (VIS, c), frm=2)
+            load("Y", "os%d" % c, [al(H)], [], lambda g, T, x: g.sync.dma_start(T.ys[:, o:o + NL], T[H][:, 0:NL]), 2.0, k)
+            load("S", "og%d" % c, [al(H)], [], lambda g, T, x: g.scalar.dma_start(T.yg[:, o:o + NL], T[H][:, NL:2 * NL]), 2.0, k)
+
+    def zsend(t):
+        u = t + 1
+        op("G", 0.1, [al("ZU%d" % t)], [], lambda g, T, x: x["send"](T["ZR%d" % u][:], T["ZU%d" % t][:], "zr%d" % u, "next"), (t, 5))
+        op("R", MIX["remote"], [al("ZU%d" % t)], [al("ZR%d" % u)], None, (t, 5), done="zr%d" % u, frm=-1)
+        V(L, [al("ZR%d" % u)], [al("ZF%d" % u)], lambda g, T, x: g.vector.tensor_copy(T["ZF%d" % u][:], T["ZR%d" % u][:]), (t, 5))
+        V(2 * L, [al("ZF%d" % u), al("ZI", u * L, u * L + L)], [al("DZ%d" % u)], lambda g, T, x: g.vector.tensor_tensor(
+            T["DZ%d" % u][:], T.ZI[:, u * L:u * L + L], T["ZF%d" % u][:], A.subtract), (t, 5))
+
+    def thresh(t):
+        n, th = "NRL%d" % t, "TH%d" % t
+        b = MIX["th"]
+        V(L, [al(n)], [al("RS", 0, 1)], lambda g, T, x: g.vector.tensor_reduce(T.RS[:, 0:1], T[n][:], AxisListType.X, A.add), (t, 0), bonus=b)
+        op("T", 0.15, [al("ON16"), al("RS", 0, 1)], [al("PB", 0, 1)], lambda g, T, x: g.tensor.matmul(T.PB[:, 0:1], T.ON16[:], T.RS[:, 0:1], True, True), (t, 0), bonus=b)
+        V(1, [al("PB", 0, 1)], [al("THI", 0, 1)], lambda g, T, x: g.vector.tensor_copy(T.THI[:, 0:1], T.PB[:, 0:1]), (t, 0), bonus=b)
+        V(1, [al("THI", 0, 1)], [al("THI", 1, 2)], lambda g, T, x: g.vector.tensor_scalar(T.THI[:, 1:2], T.THI[:, 0:1], 1, None, A.bitwise_and), (t, 0), bonus=b)
+        for j, v in ((0, 12.0), (1, -87.0)):
+            V(1, [al("THI", 1, 2)], [al(th, j, j + 1)], lambda g, T, x, j=j, v=v: g.vector.tensor_scalar(T[th][:, j:j + 1], T.THI[:, 1:2], v, None, A.add), (t, 0), bonus=b)
+
+    zsend(0)
+    for t in range(VIS):
+        for c in range(NCH):
+            walk(t, c)
+        if t:
+            if t + 1 < VIS:
+                zsend(t)
+            thresh(t)
+        for c in range(NCH):
+            epilogue(t, c)
+    return ops
+
+
+def depend(ops):
+    acc, bank = {}, {}
+    for n, o in enumerate(ops):
+        o["hard"], o["soft"] = set(), set()
+        for wr, regs in ((0, o["R"]), (1, o["W"])):
+            for b, lo, hi in regs:
+                for (m, w2, l2, h2) in acc.get(b, ()):
+                    if m != n and (wr or w2) and lo < h2 and l2 < hi:
+                        if wr and not w2 and ops[m]["q"] == o["q"] and not ops[m]["done"]:
+                            o["soft"].add(m)
+                        else:
+                            o["hard"].add(m)
+                if b in PSUM:
+                    for q, m in bank.get(b, {}).items():
+                        if m != n:
+                            (o["soft"] if q == o["q"] else o["hard"]).add(m)
+        for wr, regs in ((0, o["R"]), (1, o["W"])):
+            for b, lo, hi in regs:
+                if wr:
+                    acc[b] = [a for a in acc.get(b, []) if not (lo <= a[2] and a[3] <= hi and a[0] != n)] + [(n, 1, lo, hi)]
+                else:
+                    acc.setdefault(b, []).append((n, 0, lo, hi))
+                if b in PSUM:
+                    bank.setdefault(b, {})[o["q"]] = n
+    return ops
+
+
+def schedule(ops):
+    n = len(ops)
+    succ = [[] for _ in range(n)]
+    for i, o in enumerate(ops):
+        for m in o["hard"] | o["soft"]:
+            succ[m].append(i)
+    bot = [0.0] * n
+    hop = MIX["hop"]
+    for i in range(n - 1, -1, -1):
+        bot[i] = ops[i]["cost"] + max([bot[s] + hop for s in succ[i]], default=0.0)
+    pri = [bot[i] + ops[i]["bonus"] - MIX["skew"] * (ops[i]["key"][1] if ops[i]["key"][1] < NCH else 0) for i in range(n)]
+    need = [len(o["hard"] | o["soft"]) for o in ops]
+    ready = [0.0] * n
+    cand = {}
+    for i in range(n):
+        if not need[i]:
+            cand.setdefault(ops[i]["q"], []).append(i)
+    free, order, end = {}, [], [0.0] * n
+    start = [0.0] * n
+    while True:
+        best = None
+        for q, l in cand.items():
+            if not l:
+                continue
+            f = free.get(q, 0.0) if q != "R" else 0.0
+            lo = min(max(f, ready[i]) for i in l)
+            i = max((j for j in l if max(f, ready[j]) <= lo + MIX["slack"]), key=lambda j: (pri[j], -j))
+            s = max(f, ready[i])
+            if best is None or s < best[0]:
+                best = (s, i, q)
+        if best is None:
+            break
+        s, i, q = best
+        o = ops[i]
+        cand[q].remove(i)
+        order.append(i)
+        start[i] = s
+        end[i] = s + o["cost"]
+        free[q] = s + (0.1 if o["done"] else o["cost"])
+        for j in succ[i]:
+            need[j] -= 1
+            ready[j] = max(ready[j], end[i] + hop if i in ops[j]["hard"] else s)
+            if not need[j]:
+                cand.setdefault(ops[j]["q"], []).append(j)
+    return order, start, end
+
+
+def rank_program(g, core, T, topo):
+    rank = T.rank_of(core)
+    if rank is None:
+        return
+    ops = depend(build())
+    order, _, _ = schedule(ops)
+    place = {i: n for n, i in enumerate(order)}
+    cores = T.cores
+    to = {"next": cores[(rank + 1) % NR], "home": cores[(rank - 2) % NR]}
+    sent = [0]
+
+    def send(out, src, sem, where):
+        dst = to[where]
+        rid, pid, _ = topo.addr(dst)
+        sent[0] += len(topo.engines(core, dst))
+        return g.remote_dma(out_ap=out, in_ap=src, remote_sem=T.sem[sem], local_sem=T.sem["lsend"], pid=pid, routing_id=rid, dma_engine_mask=topo.mask(core, dst))
+
+    x = {"send": send}
+    eng = {"V": g.vector, "S": g.scalar, "T": g.tensor, "G": g, "Y": g.sync}
+    count = {q: 0 for q in eng}
+    know = {q: {} for q in eng}
+    tok, clock, sems = {}, {}, {}
+    for i in order:
+        o = ops[i]
+        q = o["q"]
+        if q == "R":
+            src = cores[(rank + o["frm"]) % NR]
+            tok[i] = (o["done"], len(topo.engines(src, core)))
+            clock[i] = {}
+            sems[o["done"]] = tok[i][1]
+            continue
+        for m in sorted((m for m in o["hard"] if m in tok), key=lambda m: -place[m]):
+            s, v = tok[m]
+            if know[q].get(s, 0) < v:
+                eng[q].wait_ge(T.sem[s], v)
+                know[q][s] = v
+                for a, b in clock[m].items():
+                    if know[q].get(a, 0) < b:
+                        know[q][a] = b
+        ins = o["f"](g, T, x)
+        clock[i] = dict(know[q])
+        if o["done"]:
+            ins.then_inc(T.sem[o["done"]], 16)
+            tok[i] = (o["done"], 16)
+            sems[o["done"]] = 16
+        elif o["W"]:
+            count[q] += 1
+            ins.then_inc(T.sem["q" + q], 1)
+            tok[i] = ("q" + q, count[q])
+            sems["q" + q] = count[q]
+    for s, v in sems.items():
+        if know["G"].get(s, 0) < v:
+            g.wait_ge(T.sem[s], v)
+    g.wait_ge(T.sem["lsend"], sent[0])

@@ -9,12 +9,13 @@ NL = L // NCH
 J = 16 * NL
 BIG = float(2 ** 22)
 LN2 = math.log(2.0)
-MIX = {"skew": 1.0, "slack": 0.12, "g": 1.5, "pe": 0.42, "hop": 0.08, "ecv": 1, "remote": 3.0, "th": 40.0, "track": 0.0, "gcov": 0.0}
+MIX = {"es": 0, "ecv": 2, "gat0": 4, "gat1": 4, "gat2": 5, "P": 38.0, "w": 2.0, "skew": 0.5, "slack": 0.02, "g": 1.5, "pe": 0.42, "hop": 0.08, "remote": 3.0, "noise": 0.0, "seed": 1,
+       "top": 60.0, "zero": 30.0, "th": 40.0, "gcov0": -5.0, "gcov1": -10.0, "gcov2": -20.0, "ch": -3.0, "tr0": 15.0, "tr1": 15.0, "tr2": 10.0, "tr3": 10.0, "tr4": 0.0, "nr": 3.0}
 
-ZM = ["PO", "TT", "MS", "G1", "G2", "CF", "NC", "W2", "UU", "CGV"] + ["E%d" % i for i in range(CL)] + ["F%d" % i for i in range(CL)]
+ZM = ["PO", "TT", "MS", "G1", "G2", "CF", "NC", "W2", "UU", "SQ"] + ["E%d" % i for i in range(CL)] + ["F%d" % i for i in range(CL)]
 ZI_ = ["MI", "XI", "CI"]
-SCALED = {"IB": 1.0, "NIB": -1.0, "I2K": 2048.0, "N2K": -2048.0, "I8K": 8192.0, "NHB": -BIG / 2, "NB": -BIG, "I16K": 16384.0, "I32B": 32.0}
-SEL = ["BOA", "BOF", "E8A", "E8F"]
+SCALED = {"IB": 1.0, "NIB": -1.0, "HA": 2.0 ** 97, "HB": -(2.0 ** 98), "I8K": 8192.0, "NHB": -BIG / 2, "NB": -BIG, "I16K": 16384.0, "I32B": 32.0}
+SEL = ["BOA", "BOF", "E8A", "E8F", "NIF"]
 
 SCRATCH = {
     "EVB": ("sbuf", [128, W], "bfloat16"), "EC": ("sbuf", [128, 2 * W], "bfloat16"), "DT": ("sbuf", [128, 2 * W], "bfloat16"),
@@ -27,7 +28,7 @@ SCRATCH = {
     "ONE": ("sbuf", [128, 128], "float32"), "I32": ("sbuf", [128, 128], "float32"),
     "ON16": ("sbuf", [128, 128], "float32"), "SEL": ("sbuf", [128, 128 * len(SEL)], "float32"), "SCN": ("sbuf", [128, 128 * len(SCALED)], "bfloat16"),
     "BO": ("sbuf", [128, 128], "bfloat16"), "BOH": ("sbuf", [128, 128], "bfloat16"), "E8": ("sbuf", [128, 128], "bfloat16"),
-    "WK": ("sbuf", [128, 2048], "bfloat16"),
+    "WK": ("sbuf", [128, 2048], "bfloat16"), "GC": ("sbuf", [128, NL], "bfloat16"),
     "KI": ("sbuf", [128, 2], "int32"), "KB": ("sbuf", [128, 2], "float32"), "RS": ("sbuf", [128, 2], "float32"), "THI": ("sbuf", [128, 4], "int32"),
     "VB": ("psum", [128, 512], "float32"), "PB": ("psum", [128, 512], "float32"),
 }
@@ -104,13 +105,13 @@ def z(T, n, c):
 def build():
     ops = []
 
-    def op(q, cost, R, Wr, f, key, done=None, frm=None, bonus=0.0):
+    def op(q, cost, R, Wr, f, key, done=None, frm=None, bonus=""):
         ops.append({"q": q, "cost": cost, "R": R, "W": Wr, "f": f, "key": key, "done": done, "frm": frm, "bonus": bonus})
 
-    def V(n, R, Wr, f, key, bonus=0.0):
+    def V(n, R, Wr, f, key, bonus=""):
         op("V", vc(n), R, Wr, f, key, bonus=bonus)
 
-    def S(n, R, Wr, f, key, bonus=0.0):
+    def S(n, R, Wr, f, key, bonus=""):
         op("S", sc(n), R, Wr, f, key, bonus=bonus)
 
     def load(q, sem, R, Wr, f, cost, key=(-1, 0)):
@@ -127,18 +128,18 @@ def build():
     load("S", "SG", [], [al("SG8")], lambda g, T, x: g.scalar.dma_start(T.SG8[0:8, :], T.sg[:]), 3.0)
     load("Y", "Z1", [], [al("ZI", L, VIS * L)], lambda g, T, x: g.sync.dma_start(T.ZI[:, L:VIS * L], T.z[:, L:VIS * L]), 10.0, (0, 9))
 
-    V(128, [], [al("ONE")], lambda g, T, x: g.vector.memset(T.ONE[:], 1.0), K0, bonus=50.0)
+    V(128, [], [al("ONE")], lambda g, T, x: g.vector.memset(T.ONE[:], 1.0), K0, bonus="top")
 
     def asel(o, i, pat, cmp, base, ch):
         oa = lambda T: T.I32[:] if o == "I32" else cst(T, o)
         ia = lambda T: T.ONE[:] if i == "ONE" else cst(T, i)
-        op("G", 0.4, [al(i)], [al(o)], lambda g, T, x: g.affine_select(oa(T), ia(T), pat, cmp, 0.0, base, ch), K0, bonus=40.0)
+        op("G", 0.4, [al(i)], [al(o)], lambda g, T, x: g.affine_select(oa(T), ia(T), pat, cmp, 0.0, base, ch), K0, bonus="top")
     asel("I32", "ONE", [[-1, 128]], A.is_equal, 0, 1)
     asel("BOA", "ONE", [[-16, 8], [0, 16]], A.is_ge, 0, 1)
     asel("BOF", "BOA", [[16, 8], [0, 16]], A.is_ge, 15, -1)
     asel("E8A", "ONE", [[1, 128]], A.is_ge, 0, -16)
     asel("E8F", "E8A", [[-1, 128]], A.is_ge, 15, 16)
-    op("G", 7.0, [], [al("DT", 0, W)], lambda g, T, x: g.iota(T.DT[:, 0:W], [[0, W]], 0, 0, allow_small_or_imprecise_dtypes=True), K0, bonus=30.0)
+    op("G", 7.0, [al("E8F"), al("BOF"), al("I32")], [al("DT", 0, W)], lambda g, T, x: g.iota(T.DT[:, 0:W], [[0, W]], 0, 0, allow_small_or_imprecise_dtypes=True), K0, bonus="zero")
     op("G", 0.15, [], [al("KI", 0, 1)], lambda g, T, x: g.iota(T.KI[:, 0:1], [[0, 1]], 0, 1), K0)
     V(1, [al("KI", 0, 1)], [al("KI", 1, 2)], lambda g, T, x: g.vector.tensor_scalar(T.KI[:, 1:2], T.KI[:, 0:1], 15, None, A.bitwise_and), (0, 8))
     V(1, [al("KI", 1, 2)], [al("KB", 0, 1)], lambda g, T, x: g.vector.tensor_scalar(T.KB[:, 0:1], T.KI[:, 1:2], -LN2, 94.0 * LN2, A.mult, A.add), (0, 8))
@@ -150,6 +151,8 @@ def build():
             T.WK[:, k * 128 + k:k * 128 + 128:16], T.SEL[:, 128 + k:256:16], F.Copy), K0)
     for n in SCALED:
         S(128, [al("I32")], [al(n)], lambda g, T, x, n=n: g.scalar.activation(cst(T, n), T.I32[:], F.Copy, scale=SCALED[n]), K0)
+    S(128, [al("I32")], [al("NIF")], lambda g, T, x: g.scalar.activation(cst(T, "NIF"), T.I32[:], F.Copy, scale=-1.0), K0)
+    V(NL, [], [al("GC")], lambda g, T, x: g.vector.memset(T.GC[:], -(2.0 ** 97)), (0, 8))
     S(128, [al("E8F")], [al("E8")], lambda g, T, x: g.scalar.activation(T.E8[:], cst(T, "E8F"), F.Copy), K0)
     S(128, [al("BOF")], [al("BO")], lambda g, T, x: g.scalar.activation(T.BO[:], cst(T, "BOF"), F.Copy), K0)
     S(128, [al("BOF")], [al("BOH")], lambda g, T, x: g.scalar.activation(T.BOH[:], cst(T, "BOF"), F.Copy, scale=0.5), K0)
@@ -157,7 +160,6 @@ def build():
     V(1, [], [al("TH0", 0, 1)], lambda g, T, x: g.vector.memset(T.TH0[:, 0:1], 12.0), (0, 8))
     V(1, [], [al("TH0", 1, 2)], lambda g, T, x: g.vector.memset(T.TH0[:, 1:2], -87.0), (0, 8))
     for c in range(NCH):
-        V(NL, [], [al("SH%d" % c, 5 * NL)], lambda g, T, x, c=c: g.vector.memset(T["SH%d" % c][:, 5 * NL:6 * NL], -1.0), (0, 8))
         V(NL, [], [al("CH%d" % c, 5 * NL)], lambda g, T, x, c=c: g.vector.memset(T["CH%d" % c][:, 5 * NL:6 * NL], 191.0), (0, 8))
 
     V(L, [al("ZI", 0, L)], [al("ZU0")], lambda g, T, x: g.vector.tensor_copy(T.ZU0[:], T.ZI[:, 0:L]), K0)
@@ -196,10 +198,10 @@ def build():
             op("S", ga(2048), R, Wr, lambda g, T, x, b=b: g.scalar.activation(
                 T.EC[:, b * 2048:b * 2048 + 2048], T.EVB[:, 0:W].indirect(T.PL[:, b * 128:b * 128 + 128]), F.Copy), (0, 4))
 
-    def fold16(bank, col, src, stop=True):
+    def fold16(bank, col, src):
         def f(g, T, x):
             for r in range(16):
-                y = g.tensor.matmul(T[bank][:, col:col + NL], T.WK[:, r * 128:r * 128 + 128], T[src][:, r:J:16], r == 0, r == 15 and stop)
+                y = g.tensor.matmul(T[bank][:, col:col + NL], T.WK[:, r * 128:r * 128 + 128], T[src][:, r:J:16], r == 0, r == 15)
             return y
         return f
 
@@ -238,57 +240,71 @@ def build():
             if i < CL:
                 op("T", pc(J), [al("WK"), al(cm)], [al(bank, 0, NL)], fold16(bank, 0, cm), k)
             if i:
-                op("T", pc(J), [al("WK"), al(dg)], [aw], fold16(bank, ACOL, dg, i == CL), k)
-            else:
-                op("T", pc(4 * NL), [al("I32"), al(Ln, 0, NL)], [aw], lambda g, T, x: g.tensor.matmul(T[bank][:, ACOL:ACOL + NL], T.I32[:], T[Ln][:, 0:NL], True, False), k)
+                op("T", pc(J), [al("WK"), al(dg)], [aw], fold16(bank, ACOL, dg), k)
             if i == CL:
-                S(NL, [aw], [al(ih, lo, hi)], lambda g, T, x, lo=lo, hi=hi: g.scalar.activation(T[ih][:, lo:hi], T[bank][:, ACOL:ACOL + NL], F.Identity, bias=-2048.0), k)
+                S(NL, [aw], [al(ih, lo, hi)], lambda g, T, x, lo=lo, hi=hi: g.scalar.activation(T[ih][:, lo:hi], T[bank][:, ACOL:ACOL + NL], F.Copy), k)
                 break
-            S(NL, [al(bank, 0, NL)], [al(sh, lo, hi)], lambda g, T, x, lo=lo, hi=hi: g.scalar.activation(T[sh][:, lo:hi], T[bank][:, 0:NL], F.Sign, bias=7.5, scale=-1.0), k)
+            if i:
+                V(NL, [al(bank, 0, NL)], [al(sh, lo, hi)], lambda g, T, x, lo=lo, hi=hi: g.vector.tensor_scalar(T[sh][:, lo:hi], T[bank][:, 0:NL], 7.5, 4096.0, A.is_lt, A.mult), k)
+                V(NL, [aw, al(sh, lo, hi)], [al(ih, lo, hi)], lambda g, T, x, lo=lo, hi=hi: g.vector.tensor_tensor(
+                    T[ih][:, lo:hi], T[bank][:, ACOL:ACOL + NL], T[sh][:, lo:hi], A.add), k)
+            else:
+                V(NL, [al(bank, 0, NL)], [al("VB", vb, vb + NL)], lambda g, T, x: g.vector.tensor_scalar(T.VB[:, vb:vb + NL], T[bank][:, 0:NL], 7.5, 4096.0, A.is_lt, A.mult), k)
+                V(NL, [al("VB", vb, vb + NL), al(Ln, 0, NL)], [al(ih, lo, hi)], lambda g, T, x, lo=lo, hi=hi: g.vector.tensor_tensor(
+                    T[ih][:, lo:hi], T.VB[:, vb:vb + NL], T[Ln][:, 0:NL], A.add), k)
+            V(NL, [al(ih, lo, hi)], [al(ix)], lambda g, T, x, lo=lo, hi=hi: g.vector.tensor_copy(T[ix][:], T[ih][:, lo:hi]), k)
             S(NL, [al(bank, 0, NL)], [al(ch, lo, hi)], lambda g, T, x, lo=lo, hi=hi, i=i: g.scalar.activation(
-                T[ch][:, lo:hi], T[bank][:, 0:NL], F.Identity, bias=32.0 * i), k)
-            op("T", pc(NL), [al("I2K"), al(sh, lo, hi)], [aw], lambda g, T, x, lo=lo, hi=hi: g.tensor.matmul(
-                T[bank][:, ACOL:ACOL + NL], cst(T, "I2K"), T[sh][:, lo:hi], False, True), k)
-            V(NL, [aw], [al(ix)], lambda g, T, x: g.vector.tensor_scalar(T[ix][:], T[bank][:, ACOL:ACOL + NL], 2048.0, None, A.add), k)
-            S(NL, [aw], [al(ih, lo, hi)], lambda g, T, x, lo=lo, hi=hi: g.scalar.activation(T[ih][:, lo:hi], T[bank][:, ACOL:ACOL + NL], F.Copy), k)
-            if i == 0:
-                op("V", ga(J), [al("EVB"), al(Un), al(ex)], [al(cg)], lambda g, T, x: g.vector.tensor_tensor(
-                    T[cg][:], T.EVB[:, 0:W].indirect(T[Un][:, NL:2 * NL]), T[ex][:], A.is_ge), k, bonus=MIX["gcov"])
-                op("T", pc(J), [al("WK"), al(cg)], [al("BM" + e, 0, NL)], fold16("BM" + e, 0, cg), k)
-                S(NL, [al("BM" + e, 0, NL)], [zr("CGV", c)], lambda g, T, x: g.scalar.activation(z(T, "CGV", c), T["BM" + e][:, 0:NL], F.Copy), k)
+                T[ch][:, lo:hi], T[bank][:, 0:NL], F.Identity, bias=32.0 * i), k, bonus="ch")
 
     def epilogue(t, c):
         k = (t, c)
         e = "%d" % c
         bm, th, Ln, ih, ch, mmn, sh = "BM" + e, "TH%d" % t, "L%d_%d" % (t, c), "IH" + e, "CH" + e, "MM" + e, "SH" + e
-        tb = MIX["track"]
+        Un, ex, cg = "US" + e, "EX" + e, "CG" + e
 
         def Z(n):
             return zr(n, c)
         bk = al(bm, 0, NL)
-        V(NL, [Z("PO"), al(th)], [Z("TT")], lambda g, T, x: g.vector.tensor_scalar(z(T, "TT", c), z(T, "PO", c), T[th][:, 1:2], 99.0, A.mult, A.add), k)
-        V(NL, [Z("CGV"), al(th)], [Z("MS")], lambda g, T, x: g.vector.tensor_scalar(z(T, "MS", c), z(T, "CGV", c), T[th][:, 0:1], None, A.is_lt), k)
+        S(NL, [Z("PO"), al(th)], [Z("TT")], lambda g, T, x: g.scalar.activation(z(T, "TT", c), z(T, "PO", c), F.Identity, bias=99.0, scale=T[th][:, 1:2]), k)
 
-        def fr(g, T, x):
-            g.tensor.matmul(T[bm][:, 0:NL], T.BO[:], z(T, "MS", c), True, False)
-            return g.tensor.matmul(T[bm][:, 0:NL], cst(T, "I32B"), z(T, "PO", c), False, True)
-        op("T", pc(2 * NL), [al("BO"), al("I32B"), Z("MS"), Z("PO")], [bk], fr, k)
-        V(NL, [bk], [Z("G1")], lambda g, T, x: g.vector.tensor_scalar(z(T, "G1", c), T[bm][:, 0:NL], 0.5, 2.0 ** 98, A.is_ge, A.mult), k)
-        V(NL, [bk], [Z("G2")], lambda g, T, x: g.vector.tensor_scalar(z(T, "G2", c), T[bm][:, 0:NL], 36.5, -(2.0 ** 99), A.is_ge, A.mult), k)
+        def gates():
+            op("V", ga(J), [al("EVB"), al(Un), al(ex)], [al(cg)], lambda g, T, x: g.vector.tensor_tensor(
+                T[cg][:], T.EVB[:, 0:W].indirect(T[Un][:, NL:2 * NL]), T[ex][:], A.is_ge), k, bonus="gcov%d" % c)
+            op("T", pc(J), [al("WK"), al(cg)], [bk], fold16(bm, 0, cg), k)
+            V(NL, [bk, al(th)], [Z("MS")], lambda g, T, x: g.vector.tensor_scalar(z(T, "MS", c), T[bm][:, 0:NL], T[th][:, 0:1], None, A.is_lt), k)
+
+            def fr(g, T, x):
+                g.tensor.matmul(T[bm][:, 0:NL], T.BO[:], z(T, "MS", c), True, False)
+                return g.tensor.matmul(T[bm][:, 0:NL], cst(T, "I32B"), z(T, "PO", c), False, True)
+            op("T", pc(2 * NL), [al("BO"), al("I32B"), Z("MS"), Z("PO")], [bk], fr, k)
+            S(NL, [bk], [Z("G1")], lambda g, T, x: g.scalar.activation(z(T, "G1", c), T[bm][:, 0:NL], F.Sign, bias=-0.5), k)
+            S(NL, [bk], [Z("G2")], lambda g, T, x: g.scalar.activation(z(T, "G2", c), T[bm][:, 0:NL], F.Sign, bias=-36.5), k)
         for i in range(CL):
+            if i == MIX["gat%d" % c]:
+                gates()
             s0, s1 = slice(i * NL, i * NL + NL), slice((i + 1) * NL, (i + 2) * NL)
-            En, Fn = "E%d" % i, "F%d" % i
+            En, Fn, tb = "E%d" % i, "F%d" % i, "tr%d" % i
 
-            def fy(g, T, x, s0=s0, s1=s1):
+            def fy(g, T, x, s0=s0, s1=s1, es=i < MIX["es"]):
                 g.tensor.matmul(T[bm][:, NL:2 * NL], cst(T, "IB"), T[ch][:, s0], True, False)
                 g.tensor.matmul(T[bm][:, NL:2 * NL], cst(T, "NIB"), z(T, "TT", c), False, True)
                 g.tensor.matmul(T[bm][:, 0:NL], T.I32[:], T[ih][:, s1], True, False)
-                g.tensor.matmul(T[bm][:, 0:NL], cst(T, "N2K"), T[sh][:, s1], False, False)
+                if s1.start < CL * NL:
+                    g.tensor.matmul(T[bm][:, 0:NL], cst(T, "NIB"), T[sh][:, s1], False, False)
+                if es:
+                    g.tensor.matmul(T[bm][:, 0:NL], cst(T, "NIF"), T[Ln][:, NL:2 * NL], False, False)
                 return g.tensor.matmul(T[bm][:, 0:NL], cst(T, "I16K"), z(T, "PO", c), False, True)
-            op("T", pc(8 * NL), [al("I32"), al("I16K"), al("N2K"), al(sh, s1.start, s1.stop), al("IB"), al("NIB"), al(ih, s1.start, s1.stop), Z("PO"), al(ch, s0.start, s0.stop), Z("TT")], [al(bm, 0, 2 * NL)], fy, k, bonus=tb)
-            V(NL, [bk, al(Ln, NL, 2 * NL)], [Z(En)], lambda g, T, x, En=En: g.vector.tensor_tensor(z(T, En, c), T[bm][:, 0:NL], T[Ln][:, NL:2 * NL], A.is_equal), k, bonus=tb)
-            S(NL, [al(bm, NL, 2 * NL)], [Z(Fn)], lambda g, T, x, Fn=Fn, i=i: g.scalar.activation(z(T, Fn, c), T[bm][:, NL:2 * NL], F.Sign, bias=0.5 - 32.0 * i), k, bonus=tb)
             last = i == CL - 1
+            es = i < MIX["es"]
+            op("T", pc((7 if last else 8) * NL + (4 * NL if es else 0)), [al("I32"), al("I16K"), al("IB"), al("NIB"), al(ih, s1.start, s1.stop), Z("PO"), al(ch, s0.start, s0.stop), Z("TT")]
+               + ([] if last else [al(sh, s1.start, s1.stop)]) + ([al("NIF"), al(Ln, NL, 2 * NL)] if es else []), [al(bm, 0, 2 * NL)], fy, k, bonus=tb)
+            if es:
+                S(NL, [bk], [Z("SQ")], lambda g, T, x: g.scalar.activation(z(T, "SQ", c), T[bm][:, 0:NL], F.Square), k, bonus=tb)
+                S(NL, [al(bm, NL, 2 * NL)], [Z(Fn)], lambda g, T, x, Fn=Fn, i=i: g.scalar.activation(z(T, Fn, c), T[bm][:, NL:2 * NL], F.Sign, bias=0.5 - 32.0 * i), k, bonus=tb)
+                S(NL, [Z("SQ")], [Z(En)], lambda g, T, x, En=En: g.scalar.activation(z(T, En, c), z(T, "SQ", c), F.Relu, bias=1.0, scale=-1.0), k, bonus=tb)
+            else:
+                V(NL, [bk, al(Ln, NL, 2 * NL)], [Z(En)], lambda g, T, x, En=En: g.vector.tensor_tensor(z(T, En, c), T[bm][:, 0:NL], T[Ln][:, NL:2 * NL], A.is_equal), k, bonus=tb)
+                S(NL, [al(bm, NL, 2 * NL)], [Z(Fn)], lambda g, T, x, Fn=Fn, i=i: g.scalar.activation(z(T, Fn, c), T[bm][:, NL:2 * NL], F.Sign, bias=0.5 - 32.0 * i), k, bonus=tb)
 
             def fw(g, T, x, s0=s0, s1=s1, En=En, Fn=Fn, last=last):
                 if last:
@@ -306,23 +322,38 @@ def build():
                 for j in range(2 if last else 1):
                     V(NL, [al(bm, j * NL, j * NL + NL), al(mmn)], [al(mmn)], lambda g, T, x, j=j: g.vector.tensor_tensor(
                         T[mmn][:], T[bm][:, j * NL:j * NL + NL], T[mmn][:], A.min), k, bonus=tb)
-        V(NL, [al(mmn)], [Z("MI")], lambda g, T, x: g.vector.tensor_scalar(z(T, "MI", c), T[mmn][:], 2048.0, None, A.add), k)
+        if MIX["gat%d" % c] == CL:
+            gates()
+        V(NL, [al(mmn)], [Z("MI")], lambda g, T, x: g.vector.tensor_copy(z(T, "MI", c), T[mmn][:]), k)
         V(NL, [Z("MI")], [Z("CI")], lambda g, T, x: g.vector.tensor_scalar(z(T, "CI", c), z(T, "MI", c), 13, 31, A.arith_shift_right, A.bitwise_and), k)
         V(NL, [Z("CI"), al(th)], [Z("NC")], lambda g, T, x: g.vector.tensor_scalar(z(T, "NC", c), z(T, "CI", c), T[th][:, 0:1], 64.0, A.is_ge, A.mult), k)
         V(NL, [Z("CI")], [Z("CF")], lambda g, T, x: g.vector.tensor_copy(z(T, "CF", c), z(T, "CI", c)), k)
         V(NL, [Z("MI")], [Z("XI")], lambda g, T, x: g.vector.tensor_scalar(z(T, "XI", c), z(T, "MI", c), 4095, None, A.bitwise_and), k)
 
         def fc(g, T, x):
+            if t + 1 < VIS:
+                bq = T[bm][:, NL:2 * NL]
+                g.tensor.matmul(bq, cst(T, "IB"), T.GC[:], True, False)
+                g.tensor.matmul(bq, cst(T, "HA"), z(T, "G1", c), False, False)
+                g.tensor.matmul(bq, cst(T, "HB"), z(T, "G2", c), False, False)
+                g.tensor.matmul(bq, T.BO[:], z(T, "NC", c), False, True)
             g.tensor.matmul(T[bm][:, 0:NL], cst(T, "IB"), z(T, "NC", c), True, False)
             return g.tensor.matmul(T[bm][:, 0:NL], cst(T, "IB"), z(T, "CF", c), False, True)
-        op("T", pc(2 * NL), [al("IB"), Z("CF"), Z("NC")], [bk], fc, k)
+        op("T", pc((2 if t + 1 == VIS else 6) * NL), [al("IB"), al("BO"), al("GC"), al("HA"), al("HB"), Z("G1"), Z("G2"), Z("CF"), Z("NC")], [al(bm, 0, 2 * NL)], fc, k)
+        o = c * NL
+        if t + 1 < VIS:
+            ns, nl = "NRS%d" % (t + 1), "NRL%d" % (t + 1)
+            V(NL, [al(bm, NL, 2 * NL)], [al(ns, o, o + NL)], lambda g, T, x: g.vector.tensor_scalar(T[ns][:, o:o + NL], T[bm][:, NL:2 * NL], 1024.0, None, A.not_equal), k, bonus="nr")
+            op("G", 0.1, [al(ns, o, o + NL)], [], lambda g, T, x: x["send"](T[nl][:, o:o + NL], T[ns][:, o:o + NL], "aN%d_%d" % (t + 1, c), "next"), k)
+            op("R", MIX["remote"], [al(ns, o, o + NL)], [al(nl, o, o + NL)], None, k, done="aN%d_%d" % (t + 1, c), frm=-1)
         S(NL, [bk, al("KB", 0, 1)], [Z("W2")], lambda g, T, x: g.scalar.activation(z(T, "W2", c), T[bm][:, 0:NL], F.Exp, bias=T.KB[:, 0:1], scale=-16.0 * LN2), k)
 
         def fs(g, T, x):
-            g.tensor.matmul(T[bm][:, 0:NL], cst(T, "IB"), z(T, "G1", c), True, False)
-            g.tensor.matmul(T[bm][:, 0:NL], cst(T, "IB"), z(T, "G2", c), False, False)
+            g.tensor.matmul(T[bm][:, 0:NL], cst(T, "IB"), T.GC[:], True, False)
+            g.tensor.matmul(T[bm][:, 0:NL], cst(T, "HA"), z(T, "G1", c), False, False)
+            g.tensor.matmul(T[bm][:, 0:NL], cst(T, "HB"), z(T, "G2", c), False, False)
             return g.tensor.matmul(T[bm][:, 0:NL], T.BOH[:], z(T, "W2", c), False, True)
-        op("T", pc(3 * NL), [al("IB"), al("BOH"), Z("G1"), Z("G2"), Z("W2")], [bk], fs, k)
+        op("T", pc(4 * NL), [al("IB"), al("GC"), al("HA"), al("HB"), al("BOH"), Z("G1"), Z("G2"), Z("W2")], [bk], fs, k)
         vb = c * 2 * NL
         r0, r1 = (vb, vb + NL), (vb + NL, vb + 2 * NL)
         Xn = "X%d_%d" % (t + 1, c)
@@ -338,12 +369,6 @@ def build():
         vt(vbs(r0), lG, vbs(r0), A.subtract, [al("VB", *r0), al(Ln, NL, 2 * NL)], [al("VB", *r0)])
         vt(vbs(r1), lambda T: z(T, "PO", c), vbs(r1), A.mult, [al("VB", *r1), Z("PO")], [al("VB", *r1)])
         vt(vbs(r1), lS, lambda T: T[Xn][:, 0:NL], A.add, [al("VB", *r1), al(Ln, 0, NL)], [al(Xn, 0, NL)])
-        o = c * NL
-        if t + 1 < VIS:
-            ns, nl = "NRS%d" % (t + 1), "NRL%d" % (t + 1)
-            V(NL, [bk], [al(ns, o, o + NL)], lambda g, T, x: g.vector.tensor_scalar(T[ns][:, o:o + NL], T[bm][:, 0:NL], 0.0, None, A.not_equal), k)
-            op("G", 0.1, [al(ns, o, o + NL)], [], lambda g, T, x: x["send"](T[nl][:, o:o + NL], T[ns][:, o:o + NL], "aN%d_%d" % (t + 1, c), "next"), k)
-            op("R", MIX["remote"], [al(ns, o, o + NL)], [al(nl, o, o + NL)], None, k, done="aN%d_%d" % (t + 1, c), frm=-1)
         V(NL, [bk, Z("W2")], [Z("UU")], lambda g, T, x: g.vector.tensor_tensor(z(T, "UU", c), T[bm][:, 0:NL], z(T, "W2", c), A.is_lt), k)
         vt(vbs(r0), lambda T: z(T, "UU", c), vbs(r0), A.mult, [al("VB", *r0), Z("UU")], [al("VB", *r0)])
         vt(vbs(r0), lG, lambda T: T[Xn][:, NL:2 * NL], A.add, [al("VB", *r0), al(Ln, NL, 2 * NL)], [al(Xn, NL, 2 * NL)])
@@ -366,7 +391,7 @@ def build():
 
     def thresh(t):
         n, th = "NRL%d" % t, "TH%d" % t
-        b = MIX["th"]
+        b = "th"
         V(L, [al(n)], [al("RS", 0, 1)], lambda g, T, x: g.vector.tensor_reduce(T.RS[:, 0:1], T[n][:], AxisListType.X, A.add), (t, 0), bonus=b)
         op("T", 0.15, [al("ON16"), al("RS", 0, 1)], [al("PB", 0, 1)], lambda g, T, x: g.tensor.matmul(T.PB[:, 0:1], T.ON16[:], T.RS[:, 0:1], True, True), (t, 0), bonus=b)
         V(1, [al("PB", 0, 1)], [al("THI", 0, 1)], lambda g, T, x: g.vector.tensor_copy(T.THI[:, 0:1], T.PB[:, 0:1]), (t, 0), bonus=b)
@@ -424,7 +449,17 @@ def schedule(ops):
     hop = MIX["hop"]
     for i in range(n - 1, -1, -1):
         bot[i] = ops[i]["cost"] + max([bot[s] + hop for s in succ[i]], default=0.0)
-    pri = [bot[i] + ops[i]["bonus"] - MIX["skew"] * (ops[i]["key"][1] if ops[i]["key"][1] < NCH else 0) for i in range(n)]
+    own = [0.0] * n
+    for i in range(n - 1, -1, -1):
+        own[i] = ops[i]["cost"] + max([own[s] + hop for s in succ[i] if ops[s]["key"] == ops[i]["key"]], default=0.0)
+    pri = []
+    for i in range(n):
+        b, (t, c) = ops[i]["bonus"], ops[i]["key"]
+        if c >= NCH or t < 0:
+            due = MIX["P"] * (t + 1) - bot[i]
+        else:
+            due = MIX["P"] * (t + 1) + MIX["skew"] * c - MIX["w"] * own[i]
+        pri.append((MIX.get(b, 0.0) if b else 0.0) - due + MIX["noise"] * ((i * 7919 + MIX["seed"] * 104729) % 1009) / 1009.0)
     need = [len(o["hard"] | o["soft"]) for o in ops]
     ready = [0.0] * n
     cand = {}
@@ -455,7 +490,7 @@ def schedule(ops):
         free[q] = s + (0.1 if o["done"] else o["cost"])
         for j in succ[i]:
             need[j] -= 1
-            ready[j] = max(ready[j], end[i] + hop if i in ops[j]["hard"] else s)
+            ready[j] = max(ready[j], end[i] + (hop if ops[j]["q"] != q else hop / 2) if i in ops[j]["hard"] else s)
             if not need[j]:
                 cand.setdefault(ops[j]["q"], []).append(j)
     return order, start, end

import math
from concourse.mybir import AluOpType, AxisListType, ActivationFunctionType

A = AluOpType
F = ActivationFunctionType
NR, W, L, VIS, CL = 8, 4096, 192, 3, 5
NCH = 3
NL = L // NCH
J = 16 * NL
BIG = float(2 ** 22)
LN2 = math.log(2.0)
MIX = {"es": 0, "ecv": 2, "gat0": 4, "gat1": 4, "gat2": 5, "P": 38.0, "w": 2.0, "skew": 0.5, "slack": 0.02, "g": 1.5, "pe": 0.42, "hop": 0.08, "remote": 3.0, "noise": 0.0, "seed": 1,
       "top": 60.0, "zero": 30.0, "th": 40.0, "gcov0": -5.0, "gcov1": -10.0, "gcov2": -20.0, "ch": -3.0, "tr0": 15.0, "tr1": 15.0, "tr2": 10.0, "tr3": 10.0, "tr4": 0.0, "nr": 3.0}

ZM = ["PO", "TT", "MS", "G1", "G2", "CF", "NC", "W2", "UU", "SQ"] + ["E%d" % i for i in range(CL)] + ["F%d" % i for i in range(CL)]
ZI_ = ["MI", "XI", "CI"]
SCALED = {"IB": 1.0, "NIB": -1.0, "HA": 2.0 ** 97, "HB": -(2.0 ** 98), "I8K": 8192.0, "NHB": -BIG / 2, "NB": -BIG, "I16K": 16384.0, "I32B": 32.0}
SEL = ["BOA", "BOF", "E8A", "E8F", "NIF"]

SCRATCH = {
    "EVB": ("sbuf", [128, W], "bfloat16"), "EC": ("sbuf", [128, 2 * W], "bfloat16"), "DT": ("sbuf", [128, 2 * W], "bfloat16"),
    "PN": ("sbuf", [128, 256], "int32"), "PT": ("sbuf", [128, 16, 16], "int32"), "PF": ("sbuf", [128, 256], "float32"),
    "TR": ("sbuf", [128, 256], "float32"), "TI": ("sbuf", [128, 256], "int32"), "TA": ("sbuf", [128, 512], "int32"),
    "PL": ("sbuf", [128, 512], "uint16"),
    "DGI": ("sbuf", [128, 1024], "int32"), "DGB": ("sbuf", [128, 1024], "bfloat16"),
    "S0I": ("sbuf", [128, L], "int32"), "G0I": ("sbuf", [128, L], "int32"), "ZI": ("sbuf", [128, VIS * L], "int32"),
    "SG8": ("sbuf", [128, VIS * L], "int32"), "SG8B": ("sbuf", [128, VIS * L], "bfloat16"), "SGB": ("sbuf", [128, VIS * L], "bfloat16"),
    "ONE": ("sbuf", [128, 128], "float32"), "I32": ("sbuf", [128, 128], "float32"),
    "ON16": ("sbuf", [128, 128], "float32"), "SEL": ("sbuf", [128, 128 * len(SEL)], "float32"), "SCN": ("sbuf", [128, 128 * len(SCALED)], "bfloat16"),
    "BO": ("sbuf", [128, 128], "bfloat16"), "BOH": ("sbuf", [128, 128], "bfloat16"), "E8": ("sbuf", [128, 128], "bfloat16"),
    "WK": ("sbuf", [128, 2048], "bfloat16"), "GC": ("sbuf", [128, NL], "bfloat16"),
    "KI": ("sbuf", [128, 2], "int32"), "KB": ("sbuf", [128, 2], "float32"), "RS": ("sbuf", [128, 2], "float32"), "THI": ("sbuf", [128, 4], "int32"),
    "VB": ("psum", [128, 512], "float32"), "PB": ("psum", [128, 512], "float32"),
}
for _t in range(VIS):
    SCRATCH["ZU%d" % _t] = ("sbuf", [128, L], "uint16")
    SCRATCH["TH%d" % _t] = ("sbuf", [128, 2], "float32")
    if _t:
        for _n, _d in (("ZR", "uint16"), ("ZF", "float32"), ("DZ", "float32"), ("NRL", "bfloat16"), ("NRS", "bfloat16")):
            SCRATCH["%s%d" % (_n, _t)] = ("sbuf", [128, L], _d)
SEMAPHORES = ["qV", "qS", "qT", "qG", "lsend", "zr1", "zr2"]
for _c in range(NCH):
    for _n, _k, _d in (("US", 2 * NL, "uint16"), ("IDX", NL, "uint16"), ("EX", J, "bfloat16"), ("CG", J, "bfloat16"), ("CM", J, "bfloat16"), ("DG", J, "bfloat16"),
                       ("IH", 6 * NL, "float32"), ("SH", 6 * NL, "bfloat16"), ("CH", 6 * NL, "bfloat16"), ("MM", NL, "float32"),
                       ("SM", NL * len(ZM), "bfloat16"), ("SI", NL * len(ZI_), "int32")):
        SCRATCH["%s%d" % (_n, _c)] = ("sbuf", [128, _k], _d)
    for _n in ("BC", "BM"):
        SCRATCH["%s%d" % (_n, _c)] = ("psum", [128, 512], "float32")
    for _t in range(VIS + 1):
        SCRATCH["L%d_%d" % (_t, _c)] = ("sbuf", [128, 2 * NL], "float32")
        if _t:
            SCRATCH["X%d_%d" % (_t, _c)] = ("sbuf", [128, 2 * NL], "float32")
            SEMAPHORES.append("aL%d_%d" % (_t, _c))
            if _t < VIS:
                SEMAPHORES.append("aN%d_%d" % (_t, _c))
DMAS = ["PTa", "PTb", "PN", "EV", "Z0", "Z1", "S0", "G0", "SG", "D0", "D1", "D2", "D3"] + ["o%s%d" % (x, c) for x in "sg" for c in range(NCH)]
SEMAPHORES += ["d_" + n for n in DMAS]
PSUM = {n for n in SCRATCH if SCRATCH[n][0] == "psum" and n != "VB"}
ACOL = 256
CY = 0.00083


def vc(n):
    return max(64, n) * CY + 0.02


def sc(n):
    return max(64, n) * CY + 0.04


def ga(n):
    return 0.055 + n * CY * MIX["g"]


def pc(cycles):
    return cycles * MIX["pe"] * 1e-3 + 0.03


def al(n, lo=0, hi=None):
    if n in SCALED:
        i = list(SCALED).index(n)
        return ("SCN", i * 128, i * 128 + 128)
    if n in SEL:
        i = SEL.index(n)
        return ("SEL", i * 128, i * 128 + 128)
    return (n, lo, SCRATCH[n][1][-1] if hi is None else hi)


def cst(T, n):
    b, lo, hi = al(n)
    return T[b][:, lo:hi]


def zr(n, c):
    b, l = ("SM", ZM) if n in ZM else ("SI", ZI_)
    i = l.index(n)
    return ("%s%d" % (b, c), i * NL, i * NL + NL)


def z(T, n, c):
    b, lo, hi = zr(n, c)
    return T[b][:, lo:hi]


def build():
    ops = []

    def op(q, cost, R, Wr, f, key, done=None, frm=None, bonus=""):
        ops.append({"q": q, "cost": cost, "R": R, "W": Wr, "f": f, "key": key, "done": done, "frm": frm, "bonus": bonus})

    def V(n, R, Wr, f, key, bonus=""):
        op("V", vc(n), R, Wr, f, key, bonus=bonus)

    def S(n, R, Wr, f, key, bonus=""):
        op("S", sc(n), R, Wr, f, key, bonus=bonus)

    def load(q, sem, R, Wr, f, cost, key=(-1, 0)):
        op(q, cost, R, Wr, f, key, done="d_" + sem)

    K0 = (-1, 0)
    for y in range(2):
        load("Y", "PT" + "ab"[y], [], [("PT", y, y + 1)], lambda g, T, x, y=y: g.sync.dma_start(T.PT[:, y:16:2, :], T.par[y:8:2, :]), 3.0)
    load("S", "S0", [], [al("S0I")], lambda g, T, x: g.scalar.dma_start(T.S0I[:], T.s0[:]), 2.4)
    load("S", "Z0", [], [al("ZI", 0, L)], lambda g, T, x: g.scalar.dma_start(T.ZI[:, 0:L], T.z[:, 0:L]), 2.4)
    load("S", "G0", [], [al("G0I")], lambda g, T, x: g.scalar.dma_start(T.G0I[:], T.g0[:]), 2.6)
    load("Y", "PN", [], [al("PN")], lambda g, T, x: g.sync.dma_start(T.PN[:], T.par[:]), 3.2)
    load("Y", "EV", [], [al("EVB")], lambda g, T, x: g.sync.dma_start(T.EVB[:], T.ev[:]), 8.0)
    load("S", "SG", [], [al("SG8")], lambda g, T, x: g.scalar.dma_start(T.SG8[0:8, :], T.sg[:]), 3.0)
    load("Y", "Z1", [], [al("ZI", L, VIS * L)], lambda g, T, x: g.sync.dma_start(T.ZI[:, L:VIS * L], T.z[:, L:VIS * L]), 10.0, (0, 9))

    V(128, [], [al("ONE")], lambda g, T, x: g.vector.memset(T.ONE[:], 1.0), K0, bonus="top")

    def asel(o, i, pat, cmp, base, ch):
        oa = lambda T: T.I32[:] if o == "I32" else cst(T, o)
        ia = lambda T: T.ONE[:] if i == "ONE" else cst(T, i)
        op("G", 0.4, [al(i)], [al(o)], lambda g, T, x: g.affine_select(oa(T), ia(T), pat, cmp, 0.0, base, ch), K0, bonus="top")
    asel("I32", "ONE", [[-1, 128]], A.is_equal, 0, 1)
    asel("BOA", "ONE", [[-16, 8], [0, 16]], A.is_ge, 0, 1)
    asel("BOF", "BOA", [[16, 8], [0, 16]], A.is_ge, 15, -1)
    asel("E8A", "ONE", [[1, 128]], A.is_ge, 0, -16)
    asel("E8F", "E8A", [[-1, 128]], A.is_ge, 15, 16)
    op("G", 7.0, [al("E8F"), al("BOF"), al("I32")], [al("DT", 0, W)], lambda g, T, x: g.iota(T.DT[:, 0:W], [[0, W]], 0, 0, allow_small_or_imprecise_dtypes=True), K0, bonus="zero")
    op("G", 0.15, [], [al("KI", 0, 1)], lambda g, T, x: g.iota(T.KI[:, 0:1], [[0, 1]], 0, 1), K0)
    V(1, [al("KI", 0, 1)], [al("KI", 1, 2)], lambda g, T, x: g.vector.tensor_scalar(T.KI[:, 1:2], T.KI[:, 0:1], 15, None, A.bitwise_and), (0, 8))
    V(1, [al("KI", 1, 2)], [al("KB", 0, 1)], lambda g, T, x: g.vector.tensor_scalar(T.KB[:, 0:1], T.KI[:, 1:2], -LN2, 94.0 * LN2, A.mult, A.add), (0, 8))
    V(2048, [], [al("DT", W, 2 * W)], lambda g, T, x: g.vector.memset(T.DT[:, W:2 * W], 0.0), K0)
    for k in range(16):
        S(128, [al("I32")], [al("WK", k * 128, k * 128 + 128)], lambda g, T, x, k=k: g.scalar.activation(T.WK[:, k * 128:k * 128 + 128], T.I32[:], F.Copy, scale=0.0), K0)
    for k in range(16):
        S(8, [al("BOF")], [al("WK", k * 128, k * 128 + 128)], lambda g, T, x, k=k: g.scalar.activation(
            T.WK[:, k * 128 + k:k * 128 + 128:16], T.SEL[:, 128 + k:256:16], F.Copy), K0)
    for n in SCALED:
        S(128, [al("I32")], [al(n)], lambda g, T, x, n=n: g.scalar.activation(cst(T, n), T.I32[:], F.Copy, scale=SCALED[n]), K0)
    S(128, [al("I32")], [al("NIF")], lambda g, T, x: g.scalar.activation(cst(T, "NIF"), T.I32[:], F.Copy, scale=-1.0), K0)
    V(NL, [], [al("GC")], lambda g, T, x: g.vector.memset(T.GC[:], -(2.0 ** 97)), (0, 8))
    S(128, [al("E8F")], [al("E8")], lambda g, T, x: g.scalar.activation(T.E8[:], cst(T, "E8F"), F.Copy), K0)
    S(128, [al("BOF")], [al("BO")], lambda g, T, x: g.scalar.activation(T.BO[:], cst(T, "BOF"), F.Copy), K0)
    S(128, [al("BOF")], [al("BOH")], lambda g, T, x: g.scalar.activation(T.BOH[:], cst(T, "BOF"), F.Copy, scale=0.5), K0)
    V(128, [], [al("ON16")], lambda g, T, x: g.vector.memset(T.ON16[:], 0.0625), (0, 8))
    V(1, [], [al("TH0", 0, 1)], lambda g, T, x: g.vector.memset(T.TH0[:, 0:1], 12.0), (0, 8))
    V(1, [], [al("TH0", 1, 2)], lambda g, T, x: g.vector.memset(T.TH0[:, 1:2], -87.0), (0, 8))
    for c in range(NCH):
        V(NL, [], [al("CH%d" % c, 5 * NL)], lambda g, T, x, c=c: g.vector.memset(T["CH%d" % c][:, 5 * NL:6 * NL], 191.0), (0, 8))

    V(L, [al("ZI", 0, L)], [al("ZU0")], lambda g, T, x: g.vector.tensor_copy(T.ZU0[:], T.ZI[:, 0:L]), K0)
    V(256, [("PT", 0, 16)], [al("PF")], lambda g, T, x: g.vector.tensor_copy(T.PF[:], T.PT[:]), K0)
    V(256, [al("PF")], [al("TR")], lambda g, T, x: g.vector.transpose(T.TR[:], T.PF[:]), K0)
    for q3 in range(8):
        V(32, [al("TR")], [("TI", q3, q3 + 1)], lambda g, T, x, q3=q3: g.vector.tensor_copy(T.TI[:, q3:256:8], T.TR[:, q3 * 32:q3 * 32 + 32]), K0)
    V(256, [al("TI")], [al("TA", 0, 256)], lambda g, T, x: g.vector.tensor_scalar(T.TA[:, 0:256], T.TI[:], 4095, None, A.bitwise_and), K0)
    V(256, [al("TI")], [al("TA", 256, 512)], lambda g, T, x: g.vector.tensor_scalar(T.TA[:, 256:512], T.TI[:], 12, None, A.logical_shift_right), K0)
    for h in range(2):
        V(256, [al("TA", h * 256, h * 256 + 256)], [al("PL", h * 256, h * 256 + 256)], lambda g, T, x, h=h: g.vector.tensor_copy(
            T.PL[:, h * 256:h * 256 + 256], T.TA[:, h * 256:h * 256 + 256]), K0)
    for b, (sh, m) in enumerate(((0, 4032), (0, 63), (12, 4032), (12, 63))):
        lo, hi = b * 256, b * 256 + 256
        if sh:
            V(256, [al("PN")], [al("DGI", lo, hi)], lambda g, T, x, lo=lo, hi=hi, sh=sh, m=m: g.vector.tensor_scalar(
                T.DGI[:, lo:hi], T.PN[:], sh, m, A.logical_shift_right, A.bitwise_and), (0, 5))
        else:
            V(256, [al("PN")], [al("DGI", lo, hi)], lambda g, T, x, lo=lo, hi=hi, m=m: g.vector.tensor_scalar(
                T.DGI[:, lo:hi], T.PN[:], m, None, A.bitwise_and), (0, 5))
    V(1024, [al("DGI")], [al("DGB")], lambda g, T, x: g.vector.tensor_copy(T.DGB[:], T.DGI[:]), (0, 5))
    for b in range(4):
        load("Y", "D%d" % b, [al("DGB", b * 256, b * 256 + 256)], [("DT", (b // 2) * W, (b // 2) * W + W)], lambda g, T, x, b=b: g.sync.dma_start(
            T.DT[b % 2:128:16, (b // 2) * W:(b // 2) * W + W], T.DGB[:, b * 256:b * 256 + 256]), 2.5, (0, 5))
    V(576, [al("SG8")], [al("SG8B")], lambda g, T, x: g.vector.tensor_copy(T.SG8B[0:8, :], T.SG8[0:8, :]), (0, 6))
    for t in range(VIS):
        op("T", 0.1, [al("E8"), al("SG8B")], [al("PB", 0, L)], lambda g, T, x, t=t: g.tensor.matmul(T.PB[:, 0:L], T.E8[0:8, :], T.SG8B[0:8, t * L:t * L + L], True, True), (t, 6))
        S(L, [al("PB", 0, L)], [al("SGB", t * L, t * L + L)], lambda g, T, x, t=t: g.scalar.activation(T.SGB[:, t * L:t * L + L], T.PB[:, 0:L], F.Copy), (t, 6))
    for b in range(4):
        R = [al("EVB"), al("PL", b * 128, b * 128 + 128)]
        Wr = [al("EC", b * 2048, b * 2048 + 2048)]
        if b < MIX["ecv"]:
            op("V", ga(2048), R, Wr, lambda g, T, x, b=b: g.vector.tensor_copy(
                T.EC[:, b * 2048:b * 2048 + 2048], T.EVB[:, 0:W].indirect(T.PL[:, b * 128:b * 128 + 128])), (0, 4))
        else:
            op("S", ga(2048), R, Wr, lambda g, T, x, b=b: g.scalar.activation(
                T.EC[:, b * 2048:b * 2048 + 2048], T.EVB[:, 0:W].indirect(T.PL[:, b * 128:b * 128 + 128]), F.Copy), (0, 4))

    def fold16(bank, col, src):
        def f(g, T, x):
            for r in range(16):
                y = g.tensor.matmul(T[bank][:, col:col + NL], T.WK[:, r * 128:r * 128 + 128], T[src][:, r:J:16], r == 0, r == 15)
            return y
        return f

    def walk(t, c):
        k = (t, c)
        o, e = c * NL, "%d" % c
        Ln, Un, ex, cm, cg, bank, dg, ix, zu = "L%d_%d" % (t, c), "US" + e, "EX" + e, "CM" + e, "CG" + e, "BC" + e, "DG" + e, "IDX" + e, "ZU%d" % t
        vb = c * 2 * NL
        if t == 0:
            for h, n in enumerate(("S0I", "G0I")):
                V(NL, [al(n, o, o + NL)], [al(Ln, h * NL, h * NL + NL)], lambda g, T, x, h=h, n=n: g.vector.tensor_copy(T[Ln][:, h * NL:h * NL + NL], T[n][:, o:o + NL]), k)
            V(NL, [al("SGB", o, o + NL)], [zr("PO", c)], lambda g, T, x: g.vector.tensor_copy(z(T, "PO", c), T.SGB[:, o:o + NL]), k)
        else:
            nr, zf, dz = "NRL%d" % t, "ZF%d" % t, "DZ%d" % t
            V(2 * NL, [al(nr, o, o + NL), al(dz, o, o + NL)], [al("VB", vb, vb + NL)], lambda g, T, x: g.vector.tensor_tensor(
                T.VB[:, vb:vb + NL], T[dz][:, o:o + NL], T[nr][:, o:o + NL], A.mult), k)
            V(NL, [al("VB", vb, vb + NL), al(zf, o, o + NL)], [al("VB", vb + NL, vb + 2 * NL)], lambda g, T, x: g.vector.tensor_tensor(
                T.VB[:, vb + NL:vb + 2 * NL], T.VB[:, vb:vb + NL], T[zf][:, o:o + NL], A.add), k)
            V(NL, [al("VB", vb + NL, vb + 2 * NL)], [al(zu, o, o + NL)], lambda g, T, x: g.vector.tensor_copy(T[zu][:, o:o + NL], T.VB[:, vb + NL:vb + 2 * NL]), k)
            op("R", MIX["remote"], [al("X%d_%d" % (t, c))], [al(Ln)], None, k, done="aL%d_%d" % (t, c), frm=-1)
            V(2 * NL, [al("SGB", t * L + o, t * L + o + NL), al(nr, o, o + NL)], [zr("PO", c)], lambda g, T, x: g.vector.tensor_tensor(
                z(T, "PO", c), T.SGB[:, t * L + o:t * L + o + NL], T[nr][:, o:o + NL], A.mult), k)
        V(2 * NL, [al(Ln)], [al(Un)], lambda g, T, x: g.vector.tensor_copy(T[Un][:], T[Ln][:]), k)
        op("S", ga(J), [al("EVB"), al(zu, o, o + NL)], [al(ex)], lambda g, T, x: g.scalar.activation(T[ex][:], T.EVB[:, 0:W].indirect(T[zu][:, o:o + NL]), F.Copy), k)
        op("V", ga(J), [al("EVB"), al(Un), al(ex)], [al(cm)], lambda g, T, x: g.vector.tensor_tensor(
            T[cm][:], T.EVB[:, 0:W].indirect(T[Un][:, 0:NL]), T[ex][:], A.is_ge), k)
        ih, ch, sh = "IH" + e, "CH" + e, "SH" + e
        aw = (bank, ACOL, ACOL + NL)
        for i in range(CL + 1):
            lo, hi = i * NL, i * NL + NL
            if i:
                if i < CL:
                    op("V", ga(J), [al("EC"), al(ix), al(ex)], [al(cm)], lambda g, T, x: g.vector.tensor_tensor(
                        T[cm][:], T.EC[:, 0:2 * W].indirect(T[ix][:]), T[ex][:], A.is_ge), k)
                op("S", ga(J), [al("DT"), al(ix)], [al(dg)], lambda g, T, x: g.scalar.activation(T[dg][:], T.DT[:, 0:2 * W].indirect(T[ix][:]), F.Copy), k)
            if i < CL:
                op("T", pc(J), [al("WK"), al(cm)], [al(bank, 0, NL)], fold16(bank, 0, cm), k)
            if i:
                op("T", pc(J), [al("WK"), al(dg)], [aw], fold16(bank, ACOL, dg), k)
            if i == CL:
                S(NL, [aw], [al(ih, lo, hi)], lambda g, T, x, lo=lo, hi=hi: g.scalar.activation(T[ih][:, lo:hi], T[bank][:, ACOL:ACOL + NL], F.Copy), k)
                break
            if i:
                V(NL, [al(bank, 0, NL)], [al(sh, lo, hi)], lambda g, T, x, lo=lo, hi=hi: g.vector.tensor_scalar(T[sh][:, lo:hi], T[bank][:, 0:NL], 7.5, 4096.0, A.is_lt, A.mult), k)
                V(NL, [aw, al(sh, lo, hi)], [al(ih, lo, hi)], lambda g, T, x, lo=lo, hi=hi: g.vector.tensor_tensor(
                    T[ih][:, lo:hi], T[bank][:, ACOL:ACOL + NL], T[sh][:, lo:hi], A.add), k)
            else:
                V(NL, [al(bank, 0, NL)], [al("VB", vb, vb + NL)], lambda g, T, x: g.vector.tensor_scalar(T.VB[:, vb:vb + NL], T[bank][:, 0:NL], 7.5, 4096.0, A.is_lt, A.mult), k)
                V(NL, [al("VB", vb, vb + NL), al(Ln, 0, NL)], [al(ih, lo, hi)], lambda g, T, x, lo=lo, hi=hi: g.vector.tensor_tensor(
                    T[ih][:, lo:hi], T.VB[:, vb:vb + NL], T[Ln][:, 0:NL], A.add), k)
            V(NL, [al(ih, lo, hi)], [al(ix)], lambda g, T, x, lo=lo, hi=hi: g.vector.tensor_copy(T[ix][:], T[ih][:, lo:hi]), k)
            S(NL, [al(bank, 0, NL)], [al(ch, lo, hi)], lambda g, T, x, lo=lo, hi=hi, i=i: g.scalar.activation(
                T[ch][:, lo:hi], T[bank][:, 0:NL], F.Identity, bias=32.0 * i), k, bonus="ch")

    def epilogue(t, c):
        k = (t, c)
        e = "%d" % c
        bm, th, Ln, ih, ch, mmn, sh = "BM" + e, "TH%d" % t, "L%d_%d" % (t, c), "IH" + e, "CH" + e, "MM" + e, "SH" + e
        Un, ex, cg = "US" + e, "EX" + e, "CG" + e

        def Z(n):
            return zr(n, c)
        bk = al(bm, 0, NL)
        S(NL, [Z("PO"), al(th)], [Z("TT")], lambda g, T, x: g.scalar.activation(z(T, "TT", c), z(T, "PO", c), F.Identity, bias=99.0, scale=T[th][:, 1:2]), k)

        def gates():
            op("V", ga(J), [al("EVB"), al(Un), al(ex)], [al(cg)], lambda g, T, x: g.vector.tensor_tensor(
                T[cg][:], T.EVB[:, 0:W].indirect(T[Un][:, NL:2 * NL]), T[ex][:], A.is_ge), k, bonus="gcov%d" % c)
            op("T", pc(J), [al("WK"), al(cg)], [bk], fold16(bm, 0, cg), k)
            V(NL, [bk, al(th)], [Z("MS")], lambda g, T, x: g.vector.tensor_scalar(z(T, "MS", c), T[bm][:, 0:NL], T[th][:, 0:1], None, A.is_lt), k)

            def fr(g, T, x):
                g.tensor.matmul(T[bm][:, 0:NL], T.BO[:], z(T, "MS", c), True, False)
                return g.tensor.matmul(T[bm][:, 0:NL], cst(T, "I32B"), z(T, "PO", c), False, True)
            op("T", pc(2 * NL), [al("BO"), al("I32B"), Z("MS"), Z("PO")], [bk], fr, k)
            S(NL, [bk], [Z("G1")], lambda g, T, x: g.scalar.activation(z(T, "G1", c), T[bm][:, 0:NL], F.Sign, bias=-0.5), k)
            S(NL, [bk], [Z("G2")], lambda g, T, x: g.scalar.activation(z(T, "G2", c), T[bm][:, 0:NL], F.Sign, bias=-36.5), k)
        for i in range(CL):
            if i == MIX["gat%d" % c]:
                gates()
            s0, s1 = slice(i * NL, i * NL + NL), slice((i + 1) * NL, (i + 2) * NL)
            En, Fn, tb = "E%d" % i, "F%d" % i, "tr%d" % i

            def fy(g, T, x, s0=s0, s1=s1, es=i < MIX["es"]):
                g.tensor.matmul(T[bm][:, NL:2 * NL], cst(T, "IB"), T[ch][:, s0], True, False)
                g.tensor.matmul(T[bm][:, NL:2 * NL], cst(T, "NIB"), z(T, "TT", c), False, True)
                g.tensor.matmul(T[bm][:, 0:NL], T.I32[:], T[ih][:, s1], True, False)
                if s1.start < CL * NL:
                    g.tensor.matmul(T[bm][:, 0:NL], cst(T, "NIB"), T[sh][:, s1], False, False)
                if es:
                    g.tensor.matmul(T[bm][:, 0:NL], cst(T, "NIF"), T[Ln][:, NL:2 * NL], False, False)
                return g.tensor.matmul(T[bm][:, 0:NL], cst(T, "I16K"), z(T, "PO", c), False, True)
            last = i == CL - 1
            es = i < MIX["es"]
            op("T", pc((7 if last else 8) * NL + (4 * NL if es else 0)), [al("I32"), al("I16K"), al("IB"), al("NIB"), al(ih, s1.start, s1.stop), Z("PO"), al(ch, s0.start, s0.stop), Z("TT")]
               + ([] if last else [al(sh, s1.start, s1.stop)]) + ([al("NIF"), al(Ln, NL, 2 * NL)] if es else []), [al(bm, 0, 2 * NL)], fy, k, bonus=tb)
            if es:
                S(NL, [bk], [Z("SQ")], lambda g, T, x: g.scalar.activation(z(T, "SQ", c), T[bm][:, 0:NL], F.Square), k, bonus=tb)
                S(NL, [al(bm, NL, 2 * NL)], [Z(Fn)], lambda g, T, x, Fn=Fn, i=i: g.scalar.activation(z(T, Fn, c), T[bm][:, NL:2 * NL], F.Sign, bias=0.5 - 32.0 * i), k, bonus=tb)
                S(NL, [Z("SQ")], [Z(En)], lambda g, T, x, En=En: g.scalar.activation(z(T, En, c), z(T, "SQ", c), F.Relu, bias=1.0, scale=-1.0), k, bonus=tb)
            else:
                V(NL, [bk, al(Ln, NL, 2 * NL)], [Z(En)], lambda g, T, x, En=En: g.vector.tensor_tensor(z(T, En, c), T[bm][:, 0:NL], T[Ln][:, NL:2 * NL], A.is_equal), k, bonus=tb)
                S(NL, [al(bm, NL, 2 * NL)], [Z(Fn)], lambda g, T, x, Fn=Fn, i=i: g.scalar.activation(z(T, Fn, c), T[bm][:, NL:2 * NL], F.Sign, bias=0.5 - 32.0 * i), k, bonus=tb)

            def fw(g, T, x, s0=s0, s1=s1, En=En, Fn=Fn, last=last):
                if last:
                    g.tensor.matmul(T[bm][:, NL:2 * NL], T.I32[:], T[ih][:, s1], True, False)
                    g.tensor.matmul(T[bm][:, NL:2 * NL], cst(T, "I8K"), T[ch][:, s1], False, True)
                g.tensor.matmul(T[bm][:, 0:NL], T.I32[:], T[ih][:, s0], True, False)
                g.tensor.matmul(T[bm][:, 0:NL], cst(T, "I8K"), T[ch][:, s0], False, False)
                g.tensor.matmul(T[bm][:, 0:NL], cst(T, "NHB"), z(T, Fn, c), False, False)
                return g.tensor.matmul(T[bm][:, 0:NL], cst(T, "NB"), z(T, En, c), False, True)
            op("T", pc((12 if last else 7) * NL), [al("I32"), al("I8K"), al("NHB"), al("NB"), al(ih, s0.start, s1.stop), al(ch, s0.start, s1.stop if last else s0.stop), Z(En), Z(Fn)],
               [al(bm, 0, 2 * NL)], fw, k, bonus=tb)
            if i == 0:
                V(NL, [bk], [al(mmn)], lambda g, T, x: g.vector.tensor_copy(T[mmn][:], T[bm][:, 0:NL]), k, bonus=tb)
            else:
                for j in range(2 if last else 1):
                    V(NL, [al(bm, j * NL, j * NL + NL), al(mmn)], [al(mmn)], lambda g, T, x, j=j: g.vector.tensor_tensor(
                        T[mmn][:], T[bm][:, j * NL:j * NL + NL], T[mmn][:], A.min), k, bonus=tb)
        if MIX["gat%d" % c] == CL:
            gates()
        V(NL, [al(mmn)], [Z("MI")], lambda g, T, x: g.vector.tensor_copy(z(T, "MI", c), T[mmn][:]), k)
        V(NL, [Z("MI")], [Z("CI")], lambda g, T, x: g.vector.tensor_scalar(z(T, "CI", c), z(T, "MI", c), 13, 31, A.arith_shift_right, A.bitwise_and), k)
        V(NL, [Z("CI"), al(th)], [Z("NC")], lambda g, T, x: g.vector.tensor_scalar(z(T, "NC", c), z(T, "CI", c), T[th][:, 0:1], 64.0, A.is_ge, A.mult), k)
        V(NL, [Z("CI")], [Z("CF")], lambda g, T, x: g.vector.tensor_copy(z(T, "CF", c), z(T, "CI", c)), k)
        V(NL, [Z("MI")], [Z("XI")], lambda g, T, x: g.vector.tensor_scalar(z(T, "XI", c), z(T, "MI", c), 4095, None, A.bitwise_and), k)

        def fc(g, T, x):
            if t + 1 < VIS:
                bq = T[bm][:, NL:2 * NL]
                g.tensor.matmul(bq, cst(T, "IB"), T.GC[:], True, False)
                g.tensor.matmul(bq, cst(T, "HA"), z(T, "G1", c), False, False)
                g.tensor.matmul(bq, cst(T, "HB"), z(T, "G2", c), False, False)
                g.tensor.matmul(bq, T.BO[:], z(T, "NC", c), False, True)
            g.tensor.matmul(T[bm][:, 0:NL], cst(T, "IB"), z(T, "NC", c), True, False)
            return g.tensor.matmul(T[bm][:, 0:NL], cst(T, "IB"), z(T, "CF", c), False, True)
        op("T", pc((2 if t + 1 == VIS else 6) * NL), [al("IB"), al("BO"), al("GC"), al("HA"), al("HB"), Z("G1"), Z("G2"), Z("CF"), Z("NC")], [al(bm, 0, 2 * NL)], fc, k)
        o = c * NL
        if t + 1 < VIS:
            ns, nl = "NRS%d" % (t + 1), "NRL%d" % (t + 1)
            V(NL, [al(bm, NL, 2 * NL)], [al(ns, o, o + NL)], lambda g, T, x: g.vector.tensor_scalar(T[ns][:, o:o + NL], T[bm][:, NL:2 * NL], 1024.0, None, A.not_equal), k, bonus="nr")
            op("G", 0.1, [al(ns, o, o + NL)], [], lambda g, T, x: x["send"](T[nl][:, o:o + NL], T[ns][:, o:o + NL], "aN%d_%d" % (t + 1, c), "next"), k)
            op("R", MIX["remote"], [al(ns, o, o + NL)], [al(nl, o, o + NL)], None, k, done="aN%d_%d" % (t + 1, c), frm=-1)
        S(NL, [bk, al("KB", 0, 1)], [Z("W2")], lambda g, T, x: g.scalar.activation(z(T, "W2", c), T[bm][:, 0:NL], F.Exp, bias=T.KB[:, 0:1], scale=-16.0 * LN2), k)

        def fs(g, T, x):
            g.tensor.matmul(T[bm][:, 0:NL], cst(T, "IB"), T.GC[:], True, False)
            g.tensor.matmul(T[bm][:, 0:NL], cst(T, "HA"), z(T, "G1", c), False, False)
            g.tensor.matmul(T[bm][:, 0:NL], cst(T, "HB"), z(T, "G2", c), False, False)
            return g.tensor.matmul(T[bm][:, 0:NL], T.BOH[:], z(T, "W2", c), False, True)
        op("T", pc(4 * NL), [al("IB"), al("GC"), al("HA"), al("HB"), al("BOH"), Z("G1"), Z("G2"), Z("W2")], [bk], fs, k)
        vb = c * 2 * NL
        r0, r1 = (vb, vb + NL), (vb + NL, vb + 2 * NL)
        Xn = "X%d_%d" % (t + 1, c)

        def vt(in0, in1, out, alu, R, Wr):
            V(NL, R, Wr, lambda g, T, x: g.vector.tensor_tensor(out(T), in0(T), in1(T), alu), k)

        def vbs(r):
            return lambda T: T.VB[:, r[0]:r[1]]
        V(NL, [Z("XI")], [al("VB", *r0)], lambda g, T, x: g.vector.tensor_copy(T.VB[:, r0[0]:r0[1]], z(T, "XI", c)), k)
        lS, lG = (lambda T: T[Ln][:, 0:NL]), (lambda T: T[Ln][:, NL:2 * NL])
        vt(vbs(r0), lS, vbs(r1), A.subtract, [al("VB", *r0), al(Ln, 0, NL)], [al("VB", *r1)])
        vt(vbs(r0), lG, vbs(r0), A.subtract, [al("VB", *r0), al(Ln, NL, 2 * NL)], [al("VB", *r0)])
        vt(vbs(r1), lambda T: z(T, "PO", c), vbs(r1), A.mult, [al("VB", *r1), Z("PO")], [al("VB", *r1)])
        vt(vbs(r1), lS, lambda T: T[Xn][:, 0:NL], A.add, [al("VB", *r1), al(Ln, 0, NL)], [al(Xn, 0, NL)])
        V(NL, [bk, Z("W2")], [Z("UU")], lambda g, T, x: g.vector.tensor_tensor(z(T, "UU", c), T[bm][:, 0:NL], z(T, "W2", c), A.is_lt), k)
        vt(vbs(r0), lambda T: z(T, "UU", c), vbs(r0), A.mult, [al("VB", *r0), Z("UU")], [al("VB", *r0)])
        vt(vbs(r0), lG, lambda T: T[Xn][:, NL:2 * NL], A.add, [al("VB", *r0), al(Ln, NL, 2 * NL)], [al(Xn, NL, 2 * NL)])
        if t + 1 < VIS:
            op("G", 0.1, [al(Xn)], [], lambda g, T, x: x["send"](T["L%d_%d" % (t + 1, c)][:], T[Xn][:], "aL%d_%d" % (t + 1, c), "next"), k)
        else:
            H = "L%d_%d" % (VIS, c)
            op("G", 0.1, [al(Xn)], [], lambda g, T, x: x["send"](T[H][:], T[Xn][:], "aL%d_%d" % (VIS, c), "home"), k)
            op("R", MIX["remote"], [al(Xn)], [al(H)], None, k, done="aL%d_%d" % (VIS, c), frm=2)
            load("Y", "os%d" % c, [al(H)], [], lambda g, T, x: g.sync.dma_start(T.ys[:, o:o + NL], T[H][:, 0:NL]), 2.0, k)
            load("S", "og%d" % c, [al(H)], [], lambda g, T, x: g.scalar.dma_start(T.yg[:, o:o + NL], T[H][:, NL:2 * NL]), 2.0, k)

    def zsend(t):
        u = t + 1
        op("G", 0.1, [al("ZU%d" % t)], [], lambda g, T, x: x["send"](T["ZR%d" % u][:], T["ZU%d" % t][:], "zr%d" % u, "next"), (t, 5))
        op("R", MIX["remote"], [al("ZU%d" % t)], [al("ZR%d" % u)], None, (t, 5), done="zr%d" % u, frm=-1)
        V(L, [al("ZR%d" % u)], [al("ZF%d" % u)], lambda g, T, x: g.vector.tensor_copy(T["ZF%d" % u][:], T["ZR%d" % u][:]), (t, 5))
        V(2 * L, [al("ZF%d" % u), al("ZI", u * L, u * L + L)], [al("DZ%d" % u)], lambda g, T, x: g.vector.tensor_tensor(
            T["DZ%d" % u][:], T.ZI[:, u * L:u * L + L], T["ZF%d" % u][:], A.subtract), (t, 5))

    def thresh(t):
        n, th = "NRL%d" % t, "TH%d" % t
        b = "th"
        V(L, [al(n)], [al("RS", 0, 1)], lambda g, T, x: g.vector.tensor_reduce(T.RS[:, 0:1], T[n][:], AxisListType.X, A.add), (t, 0), bonus=b)
        op("T", 0.15, [al("ON16"), al("RS", 0, 1)], [al("PB", 0, 1)], lambda g, T, x: g.tensor.matmul(T.PB[:, 0:1], T.ON16[:], T.RS[:, 0:1], True, True), (t, 0), bonus=b)
        V(1, [al("PB", 0, 1)], [al("THI", 0, 1)], lambda g, T, x: g.vector.tensor_copy(T.THI[:, 0:1], T.PB[:, 0:1]), (t, 0), bonus=b)
        V(1, [al("THI", 0, 1)], [al("THI", 1, 2)], lambda g, T, x: g.vector.tensor_scalar(T.THI[:, 1:2], T.THI[:, 0:1], 1, None, A.bitwise_and), (t, 0), bonus=b)
        for j, v in ((0, 12.0), (1, -87.0)):
            V(1, [al("THI", 1, 2)], [al(th, j, j + 1)], lambda g, T, x, j=j, v=v: g.vector.tensor_scalar(T[th][:, j:j + 1], T.THI[:, 1:2], v, None, A.add), (t, 0), bonus=b)

    zsend(0)
    for t in range(VIS):
        for c in range(NCH):
            walk(t, c)
        if t:
            if t + 1 < VIS:
                zsend(t)
            thresh(t)
        for c in range(NCH):
            epilogue(t, c)
    return ops


def depend(ops):
    acc, bank = {}, {}
    for n, o in enumerate(ops):
        o["hard"], o["soft"] = set(), set()
        for wr, regs in ((0, o["R"]), (1, o["W"])):
            for b, lo, hi in regs:
                for (m, w2, l2, h2) in acc.get(b, ()):
                    if m != n and (wr or w2) and lo < h2 and l2 < hi:
                        if wr and not w2 and ops[m]["q"] == o["q"] and not ops[m]["done"]:
                            o["soft"].add(m)
                        else:
                            o["hard"].add(m)
                if b in PSUM:
                    for q, m in bank.get(b, {}).items():
                        if m != n:
                            (o["soft"] if q == o["q"] else o["hard"]).add(m)
        for wr, regs in ((0, o["R"]), (1, o["W"])):
            for b, lo, hi in regs:
                if wr:
                    acc[b] = [a for a in acc.get(b, []) if not (lo <= a[2] and a[3] <= hi and a[0] != n)] + [(n, 1, lo, hi)]
                else:
                    acc.setdefault(b, []).append((n, 0, lo, hi))
                if b in PSUM:
                    bank.setdefault(b, {})[o["q"]] = n
    return ops


def schedule(ops):
    n = len(ops)
    succ = [[] for _ in range(n)]
    for i, o in enumerate(ops):
        for m in o["hard"] | o["soft"]:
            succ[m].append(i)
    bot = [0.0] * n
    hop = MIX["hop"]
    for i in range(n - 1, -1, -1):
        bot[i] = ops[i]["cost"] + max([bot[s] + hop for s in succ[i]], default=0.0)
    own = [0.0] * n
    for i in range(n - 1, -1, -1):
        own[i] = ops[i]["cost"] + max([own[s] + hop for s in succ[i] if ops[s]["key"] == ops[i]["key"]], default=0.0)
    pri = []
    for i in range(n):
        b, (t, c) = ops[i]["bonus"], ops[i]["key"]
        if c >= NCH or t < 0:
            due = MIX["P"] * (t + 1) - bot[i]
        else:
            due = MIX["P"] * (t + 1) + MIX["skew"] * c - MIX["w"] * own[i]
        pri.append((MIX.get(b, 0.0) if b else 0.0) - due + MIX["noise"] * ((i * 7919 + MIX["seed"] * 104729) % 1009) / 1009.0)
    need = [len(o["hard"] | o["soft"]) for o in ops]
    ready = [0.0] * n
    cand = {}
    for i in range(n):
        if not need[i]:
            cand.setdefault(ops[i]["q"], []).append(i)
    free, order, end = {}, [], [0.0] * n
    start = [0.0] * n
    while True:
        best = None
        for q, l in cand.items():
            if not l:
                continue
            f = free.get(q, 0.0) if q != "R" else 0.0
            lo = min(max(f, ready[i]) for i in l)
            i = max((j for j in l if max(f, ready[j]) <= lo + MIX["slack"]), key=lambda j: (pri[j], -j))
            s = max(f, ready[i])
            if best is None or s < best[0]:
                best = (s, i, q)
        if best is None:
            break
        s, i, q = best
        o = ops[i]
        cand[q].remove(i)
        order.append(i)
        start[i] = s
        end[i] = s + o["cost"]
        free[q] = s + (0.1 if o["done"] else o["cost"])
        for j in succ[i]:
            need[j] -= 1
            ready[j] = max(ready[j], end[i] + (hop if ops[j]["q"] != q else hop / 2) if i in ops[j]["hard"] else s)
            if not need[j]:
                cand.setdefault(ops[j]["q"], []).append(j)
    return order, start, end


def rank_program(g, core, T, topo):
    rank = T.rank_of(core)
    if rank is None:
        return
    ops = depend(build())
    order, _, _ = schedule(ops)
    place = {i: n for n, i in enumerate(order)}
    cores = T.cores
    to = {"next": cores[(rank + 1) % NR], "home": cores[(rank - 2) % NR]}
    sent = [0]

    def send(out, src, sem, where):
        dst = to[where]
        rid, pid, _ = topo.addr(dst)
        sent[0] += len(topo.engines(core, dst))
        return g.remote_dma(out_ap=out, in_ap=src, remote_sem=T.sem[sem], local_sem=T.sem["lsend"], pid=pid, routing_id=rid, dma_engine_mask=topo.mask(core, dst))

    x = {"send": send}
    eng = {"V": g.vector, "S": g.scalar, "T": g.tensor, "G": g, "Y": g.sync}
    count = {q: 0 for q in eng}
    know = {q: {} for q in eng}
    tok, clock, sems = {}, {}, {}
    for i in order:
        o = ops[i]
        q = o["q"]
        if q == "R":
            src = cores[(rank + o["frm"]) % NR]
            tok[i] = (o["done"], len(topo.engines(src, core)))
            clock[i] = {}
            sems[o["done"]] = tok[i][1]
            continue
        for m in sorted((m for m in o["hard"] if m in tok), key=lambda m: -place[m]):
            s, v = tok[m]
            if know[q].get(s, 0) < v:
                eng[q].wait_ge(T.sem[s], v)
                know[q][s] = v
                for a, b in clock[m].items():
                    if know[q].get(a, 0) < b:
                        know[q][a] = b
        ins = o["f"](g, T, x)
        clock[i] = dict(know[q])
        if o["done"]:
            ins.then_inc(T.sem[o["done"]], 16)
            tok[i] = (o["done"], 16)
            sems[o["done"]] = 16
        elif o["W"]:
            count[q] += 1
            ins.then_inc(T.sem["q" + q], 1)
            tok[i] = ("q" + q, count[q])
            sems["q" + q] = count[q]
    for s, v in sems.items():
        if know["G"].get(s, 0) < v:
            g.wait_ge(T.sem[s], v)
    g.wait_ge(T.sem["lsend"], sent[0])
